import numpy as np, ml_dtypes
CORES = [1,5,17,21,33,37,49,53]
N = 8
BF = ml_dtypes.bfloat16
def gentries(a):
    return np.ascontiguousarray(a.reshape(8, 16, -1).transpose(0, 2, 1)).reshape(8, -1)
def gtable(e):
    e = np.asarray(e); return np.ascontiguousarray(e.reshape(8, -1, 16).transpose(0, 2, 1)).reshape(128, -1).astype(np.int32)
V, A, W, M, RO, ST = 1536, 512, 3072, 4096, 3, 1
H, E, Z = V - A, W - 1, M - 1
def parts(rng):
    a = rng.choice(np.array([1, 2, 4, 8]), (8, 16, 1)); b = rng.choice(np.array([15, 63, 255]), (8, 16, 1))
    e = rng.integers(-a, a + 1, (8, 16, W)); c = rng.integers(-b, b + 1, (8, 16, M)); m = rng.integers(0, M, (8, 2, W))
    share = rng.permutation(np.linspace(0.42, 0.7, 8)).reshape(8, 1, 1)
    k = np.where(rng.random((8, 2, M)) < share, rng.integers(0, E, (8, 2, M)), E)
    fill = rng.choice(np.array([0.9, 0.97, 1.0]), (N, 8, 1))
    p = np.where(rng.random((N, 8, V)) < fill, rng.integers(0, E, (N, 8, V)), E)
    return p, e, m, c, k
def lone(rng):
    return np.where(np.arange(2)[:, None] == rng.integers(0, 2, M), rng.integers(0, E, (2, M)), E)
def alike(x):
    return np.ascontiguousarray(np.broadcast_to(x, (N,) + x.shape))
def pack(p, e, m, c, k):
    e[:, :, E] = 0; m[:, :, E] = Z; k[:, :, Z] = E
    return {"todo": np.stack([gtable(a) for a in p]), "eff": alike(e.reshape(128, W).astype(np.float32).astype(BF)),
            "meth": alike((m[:, 0] + 4096 * m[:, 1]).astype(np.int32)), "pre": alike(c.reshape(128, M).astype(np.float32).astype(BF)),
            "kid": alike((k[:, 0] + 4096 * k[:, 1]).astype(np.int32))}
def setup_inputs(rng):
    return pack(*parts(rng))
def setup_inputs_room(rng):
    p, e, m, c, k = parts(rng)
    m = 3 * rng.integers(0, (M - 1) // 3, (8, 2, W)) + np.arange(W) % 3
    k = rng.integers(0, E, (8, 2, M)); one = rng.integers(0, 2, (8, M)); cl = np.arange(M) % 3
    k[:, 0] = np.where((cl == 0) | ((cl == 1) & (one == 0)), E, k[:, 0]); k[:, 1] = np.where((cl == 0) | ((cl == 1) & (one == 1)), E, k[:, 1])
    for q in range(N):
        for g in range(8):
            n = int(rng.choice(np.array([0, 1, H - 1, H, H + 1, V - 1, V, V + 1, 2 * V])))
            if q == 0: n = (V, V + 1, V - 1, H, H + 1, H - 1, 2 * V, 1)[g]
            n2 = int(rng.integers(max(0, n - V), n // 2 + 1)); n1 = n - 2 * n2; n0 = V - n1 - n2
            kinds = rng.permutation(np.repeat(np.array([0, 1, 2]), np.array([n0, n1, n2])))
            t = 3 * rng.integers(0, (W - 1) // 3, V) + kinds
            p[q, g] = np.where((kinds == 0) & (rng.random(V) < 0.3), E, t)
    return pack(p, e, m, c, k)
def setup_inputs_ties(rng):
    p, e, m, c, k = parts(rng)
    e[::2] = rng.integers(-1, 2, (4, 16, W)) * (rng.random((4, 16, W)) < 0.01)
    c[::2] = rng.integers(-2, 3, (4, 16, M))
    m[::2, 1] = np.where(rng.random((4, W)) < 0.3, m[::2, 0], m[::2, 1])
    m[1::2, 1] = m[1::2, 0] ^ 1
    c[1::2, :, 1::2] = c[1::2, :, 0::2]; i = int(rng.integers(0, 16))
    c[1::2, i, 1::2] = rng.integers(-255, 256, (4, M // 2))
    return pack(p, e, m, c, k)
def setup_inputs_ends(rng):
    p, e, m, c, k = parts(rng)
    e[0] = 8; e[1] = -8
    p[:, :2] = rng.integers(0, E, (N, 2, V)); m[:2] = rng.integers(0, Z, (2, 2, W)); c[:2] = rng.integers(-255, 256, (2, 16, M))
    k[0] = lone(rng); k[1] = lone(rng)
    c[2] = rng.choice(np.array([-255, 255, 0]), (16, M))
    p[:, 3] = rng.choice(np.array([0, 1, E - 1, E]), (N, V))
    m[4] = rng.choice(np.array([0, 1, M - 2, Z]), (2, W)); k[4][:, [0, 1, M - 2]] = rng.integers(0, E, (2, 3))
    k[5] = rng.choice(np.array([0, 1, E - 1, E]), (2, M))
    t = rng.permutation(E)[:2]; u = rng.permutation(Z)[:2]
    p[:, 6] = t[0]; m[6, 0, t[0]] = u[0]; m[6, 1, t[0]] = u[1]
    k[6, 0, u[0]] = t[0]; k[6, 1, u[0]] = t[1]; k[6, 0, u[1]] = t[1]; k[6, 1, u[1]] = E
    sg = rng.permutation(np.repeat(np.array([-1, 1]), 8))[:, None]
    e[7] = sg * 8 * (1 - 2 * (np.arange(W) % 2))
    p[:, 7] = 2 * rng.integers(0, E // 2, (N, V)) + (np.arange(N * V).reshape(N, V) >= N * V // 2 + 15)
    m[7, 0] = 2 * rng.integers(0, M // 2, W); m[7, 1] = 2 * rng.integers(0, M // 2 - 1, W) + 1; k[7] = lone(rng)
    lo = rng.integers(-255, 101, (16, M)); hi = rng.integers(-100, 256, (16, M))
    c[7] = np.where(np.arange(M) % 2 == 1, np.where(sg > 0, lo, -255), np.where(sg > 0, 255, hi))
    return pack(p, e, m, c, k)
def setup_inputs_thin(rng):
    p, e, m, c, k = parts(rng); p = rng.integers(0, E, (N, 8, V))
    fill = rng.choice(np.array([0.0, 0.02, 0.3, 1.0]), (N, 8, 1)); o = rng.permutation(8)
    fill[int(rng.integers(0, N))] = 0.0; fill[:, o[0]] = 0.0; fill[:, o[1:3]] = 1.0
    p = np.where(rng.random((N, 8, V)) < fill, p, E); p[:, o[3], :V // 2] = E
    g = int(o[4]); q = int(rng.integers(0, N - 1)); cl = np.arange(M) % 3
    m[g] = 3 * rng.integers(0, (M - 1) // 3, (2, W)) + np.arange(W) % 3
    one = np.arange(2)[:, None] == rng.integers(0, 2, M); leaf = 3 * rng.integers(0, E // 3, (2, M)); go = 3 * rng.integers(0, E // 3, (2, M)) + 2
    k[g] = np.where(cl == 1, leaf, np.where((cl == 2) & one, go, E))
    kinds = np.full(N, 2); kinds[[q - 1, q]] = 1
    p[:, g] = 3 * rng.integers(0, E // 3, (N, V)) + kinds[:, None]; p[(q + 2) % N, g] = E
    return pack(p, e, m, c, k)
def setup_inputs_spread(rng):
    p, e, m, c, k = parts(rng)
    o = np.stack([rng.permutation(E) for g in range(8)]); gi = np.arange(8)
    p = np.where(rng.random((N, 8, V)) < 0.97, o[gi[None, :, None], (E * rng.random((N, 8, V)) ** 4).astype(np.int64)], E)
    k = np.where(k == E, E, o[gi[:, None, None], (E * rng.random((8, 2, M)) ** 3).astype(np.int64)])
    s = rng.choice(np.array([-1, 1]), (8, 16, W)); e = s * np.minimum(8, np.floor(np.exp2(3.2 * rng.random((8, 1, W))) * rng.random((8, 16, W)) + 0.5)).astype(np.int64) * (rng.random((8, 1, W)) > 0.0625)
    s = rng.choice(np.array([-1, 1]), (8, 16, M)); c = s * np.minimum(255, np.floor(np.exp2(8 * rng.random((8, 16, M))))).astype(np.int64)
    w = int(rng.integers(0, 8)); a = rng.choice(np.array([-1, 1]), (16, 1)) * rng.integers(3, 8, (16, 1))
    e[w] = a * np.array([0, 1, -1])[np.arange(W) % 3] + rng.integers(-1, 2, (16, W)); c[w] = rng.integers(-127, 128, (16, M))
    m[w] = rng.integers(0, Z, (2, W)); k[w] = lone(rng)
    kinds = np.zeros((N, V), np.int64); kinds[0::2, V // 2:] = 1; kinds[1::2, :V // 2] = 2
    p[:, w] = 3 * rng.integers(0, E // 3, (N, V)) + kinds
    return pack(p, e, m, c, k)
def check_inputs(d):
    bad = []
    if np.min(d["todo"]) < 0 or np.max(d["todo"]) > E: bad.append("range of todo")
    for nm, hi in (("eff", 8), ("pre", 255)):
        x = np.asarray(d[nm]).astype(np.float32)
        if not np.all((x >= -hi) & (x <= hi) & (x == np.rint(x))): bad.append("whole numbers in range: " + nm)
    for nm, hi in (("meth", Z), ("kid", E)):
        x = np.asarray(d[nm]).astype(np.int64)
        if not np.all((x >= 0) & ((x & 4095) <= hi) & ((x >> 12) <= hi)): bad.append("range of " + nm)
    for nm in ("eff", "meth", "pre", "kid"):
        x = np.asarray(d[nm]).astype(np.float64)
        if not np.all(x == x[:1]): bad.append("not alike on all ranks: " + nm)
    if not np.all(np.asarray(d["eff"])[:, :, E].astype(np.float32) == 0): bad.append("effects of the empty type")
    if not np.all(np.asarray(d["meth"])[:, :, E] == Z + 4096 * Z): bad.append("methods of the empty type")
    if not np.all(np.asarray(d["kid"])[:, :, Z] == E + 4096 * E): bad.append("kids of the empty method")
    return bad
def reference(todo, eff, meth, pre, kid):
    p = np.stack([gentries(a) for a in todo]).astype(np.int64)
    ef = eff.astype(np.float32).astype(np.int64).reshape(N, 8, 16, W); pr = pre.astype(np.float32).astype(np.int64).reshape(N, 8, 16, M)
    me = meth.astype(np.int64); ki = kid.astype(np.int64)
    for rnd in range(RO):
        e = np.take_along_axis(ef, p[:, :, None, :], 3)
        line = np.ascontiguousarray(e.transpose(1, 2, 0, 3)).reshape(8, 16, N * V)
        st = (np.add.accumulate(line, axis=2) - line).reshape(8, 16, N, V).transpose(2, 0, 1, 3)
        m = np.take_along_axis(me, p, 2); m0 = m & 4095; m1 = m >> 12
        c0 = np.add.reduce((st >= np.take_along_axis(pr, m0[:, :, None, :], 3)).astype(np.int64), axis=2)
        c1 = np.add.reduce((st >= np.take_along_axis(pr, m1[:, :, None, :], 3)).astype(np.int64), axis=2)
        k = np.take_along_axis(ki, np.where(c1 > c0, m1, m0), 2)
        kk = np.stack([k & 4095, k >> 12], axis=-1).reshape(N, 8, 2 * V)
        row = np.full((N, 8, V), E, np.int64)
        for a in range(N):
            for g in range(8):
                v = kk[a, g][kk[a, g] != E][:V]; row[a, g, :len(v)] = v
        p = np.concatenate([np.roll(row[:, :, H:], 1, axis=0), row[:, :, :H]], axis=2)
    return {"yp": np.stack([gtable(a) for a in p]).astype(np.float32), "ys": np.ascontiguousarray(st.reshape(N, 128, V)[:, :, ::ST]).astype(np.float32)}

@@ -1,0 +1,519 @@
+from concourse.bass import DstId, RemoteDMATransfer
+from concourse.mybir import AluOpType, ActivationFunctionType
+
+ALU = AluOpType
+ACT = ActivationFunctionType
+N, V, A, W, M, RO = 8, 1536, 512, 3072, 4096, 3
+H = V - A
+EMPTY = W - 1
+CH = 128
+NCH = V // CH
+NP = V // 2
+WREAD = V + 16
+WDUMMY = 2 * V + 16
+WCOLS = WDUMMY + NP
+KEY0 = 1024
+KEYADD = KEY0 + 13
+RND = 12582912.0
+MH = M // 2
+F32, BF, F16, I32, U16 = "float32", "bfloat16", "float16", "int32", "uint16"
+
+SCRATCH = {k: ("sbuf", [128, n], d) for d, names in (
+    (I32, dict(TD=96, KC=128, K2=256, MC=192, M2=768, CI=4)),
+    (BF, dict(MD=768, DG=512, ST=MH, ZS=256, EF=W, PC=M, MT=W, TT=M, IX=160,
+              ZO=144, ZM0=144, ZM1=144, Z1=148, Z2=148, ZT=148, LT=768, ZA=144, ZB=144, ZC=144, ZE=144, PA=136, PB=136,
+              ID=128, NI=128, MK=H, ET=A + 2, EH=H + 2, EJ=A, MG=V, P1=V, B0=V, B1=V, GA=NP + 2, GB=NP + 2,
+              W0=WCOLS, W1=WCOLS)),
+    (F32, dict(CF=4, CX=48, CD=48, CC=32, TG=8, TG0=8, TI=2, TI0=2, ZR=32, TH=96, YP=128, YS=V, MF=96, VT=96, VD=96,
+               CE=48, OF=48, SM=8, LB0=32, LB1=32, LB2=32, BS=32, BX=16, UF=256, IF=128)),
+    (F16, dict(SR=V, D0=V, MS=96, KS=NP + 2)),
+    (U16, dict(TL0=128, TL1=128, TL2=128, MU=192, AB=96, OU=48)),
+) for k, n in names.items()}
+PSUM_KEYS = ("pd0", "pd1", "pd2", "pmh", "pmt", "px", "py", "pz")
+SCRATCH.update({k: ("psum", [128, 512], F32) for k in PSUM_KEYS})
+SEMAPHORES = ["cv", "cs", "ct", "cg", "sent",
+              "dtd", "dkc", "dmc", "def", "dpc", "dmt", "dys0", "dys1", "dys2", "dyp", "ttx",
+              "tail1", "tail2", "tail3", "sum0", "sum1", "sum2"]
+
+
+def sum_senders(rnd, dst):
+    if dst == 0:
+        return []
+    s = [dst - 1] + list(range(dst - 1))
+    if rnd > 0 and dst < N - 1:
+        s.append(N - 1)
+    return s
+
+
+def bits(engines):
+    m = 0
+    for e in engines:
+        m |= 1 << e
+    return m
+
+
+def rank_program(g, core, T, topo):
+    rank = T.rank_of(core)
+    if rank is None:
+        return
+    cores = T.cores
+    Q = {"v": g.vector, "s": g.scalar, "t": g.tensor, "g": g, "y": g.sync}
+    own = {"v": "cv", "s": "cs", "t": "ct", "g": "cg"}
+    count = {}
+    seen = {q: {} for q in Q}
+    writer, readers = {}, {}
+
+    def wait(q, toks):
+        need = {}
+        for s, v in toks:
+            if v > seen[q].get(s, 0) and v > need.get(s, 0):
+                need[s] = v
+        for s, v in need.items():
+            Q[q].wait_ge(T.sem[s], v)
+            seen[q][s] = v
+
+    def before(q, rd, wr):
+        toks = []
+        for k in rd:
+            toks += writer.get(k, [])
+            if k in PSUM_KEYS:
+                toks += [t for t in readers.get(k, []) if t[0] != own.get(q)]
+        for k in wr:
+            toks += writer.get(k, []) + readers.get(k, [])
+        wait(q, toks)
+
+    def after(tok, rd, wr):
+        for k in rd:
+            readers.setdefault(k, []).append(tok)
+        for k in wr:
+            writer[k] = [tok]
+            readers[k] = []
+
+    def op(q, rd, wr, fn):
+        before(q, rd, wr)
+        s = own[q]
+        fn().then_inc(T.sem[s], 1)
+        count[s] = count.get(s, 0) + 1
+        after((s, count[s]), rd, wr)
+
+    def dmas(q, s, rd, wr, pairs):
+        before(q, rd, wr)
+        for o, i in pairs:
+            Q[q].dma_start(o, i).then_inc(T.sem[s], 16)
+        count[s] = count.get(s, 0) + 16 * len(pairs)
+        after((s, count[s]), rd, wr)
+
+    def mm(rd, wr, *groups, first=True, last=True):
+        def run():
+            for items in groups:
+                for n, (o, l, r) in enumerate(items):
+                    ins = g.tensor.matmul(o, l, r, first and n == 0, last and n == len(items) - 1)
+            return ins
+        op("t", rd, wr, run)
+
+    def ts(rd, wr, out, in0, s1, op0, s2=None, op1=None):
+        if op1 is None:
+            op("v", rd, wr, lambda: g.vector.tensor_scalar(out, in0, s1, None, op0))
+        else:
+            op("v", rd, wr, lambda: g.vector.tensor_scalar(out, in0, s1, s2, op0, op1))
+
+    def tt(rd, wr, out, in0, in1, o):
+        op("v", rd, wr, lambda: g.vector.tensor_tensor(out, in0, in1, o))
+
+    def cp(rd, wr, out, in_):
+        op("v", rd, wr, lambda: g.vector.tensor_copy(out, in_))
+
+    def fill(wr, ap, c):
+        op("v", [], wr, lambda: g.vector.memset(ap, c))
+
+    def act(rd, wr, out, in_, f, **kw):
+        op("s", rd, wr, lambda: g.scalar.activation(out, in_, f, **kw))
+
+    def copy(q, rd, wr, out, in_, **kw):
+        if q == "v":
+            cp(rd, wr, out, in_)
+        else:
+            act(rd, wr, out, in_, ACT.Copy, **kw)
+
+    far = topo.engines(core, next(c for c in cores if topo.chip(c) != topo.chip(core)))
+    mate = next(r for r in range(N) if r != rank and topo.chip(cores[r]) == topo.chip(core))
+    whole = topo.engines(core, cores[mate])
+    near = [e for e in whole if e not in far]
+    half = 0 if rank < mate else 1
+
+    def engines_to(r):
+        return near if r == mate else far
+
+    def arrival(s, n, key):
+        count[s] = n
+        writer[key] = [(s, n)]
+
+    def send(rd, src, dsts, s, engines=None):
+        if not dsts:
+            return
+        before("g", rd, [])
+        if len(dsts) == 1:
+            e = engines or engines_to(dsts[0][0])
+            rid, pid, _ = topo.addr(cores[dsts[0][0]])
+            g.remote_dma(dsts[0][1], src, T.sem[s], T.sem["sent"], pid, rid, bits(e))
+            count["sent"] = count.get("sent", 0) + len(e)
+            return
+        tr = []
+        for x in ([d for d in dsts if d[0] != mate], [d for d in dsts if d[0] == mate]):
+            if x:
+                e = engines_to(x[0][0])
+                tr.append(RemoteDMATransfer(dst_ids=[DstId(rid=topo.addr(cores[r])[0], pnc=topo.addr(cores[r])[1]) for r, _ in x],
+                                            dma_engine_mask=bits(e), remote_sem=T.sem[s], src=src, dsts=[ap for _, ap in x]))
+                count["sent"] = count.get("sent", 0) + len(e)
+        g.remote_dma_fused(tr, local_sem=T.sem["sent"])
+
+    TL = [T.TL0, T.TL1, T.TL2, T.YP]
+    LB = [T.LB0, T.LB1, T.LB2]
+    WN = [T.W0, T.W1]
+    PD = [T.pd0, T.pd1, T.pd2]
+    for r in range(RO):
+        arrival("tail%d" % (r + 1), len(engines_to((rank - 1) % N)), "TLt%d" % (r + 1))
+        if sum_senders(r, rank):
+            arrival("sum%d" % r, sum(len(engines_to(x)) for x in sum_senders(r, rank)), "LBr%d" % r)
+    arrival("ttx", len(whole), "TTx")
+    mine = slice(MH * half, MH * half + MH)
+
+    dmas("s", "dmc", [], ["MC"], [(T.MC[:], T.meth[:])])
+    dmas("y", "dtd", [], ["TD"], [(T.TD[:], T.todo[:])])
+    dmas("s", "dkc", [], [], [(T.KC[j:128:8, :], T.kid[j, mine]) for j in range(4)])
+    dmas("y", "dkc", [], ["KC"], [(T.KC[j:128:8, :], T.kid[j, mine]) for j in range(4, 8)])
+    dmas("y", "def", [], ["EF"], [(T.EF[:], T.eff[:])])
+
+    op("g", [], ["CI0"], lambda: g.iota(T.CI[:, 0:1], [[1, 1]], 0, 1))
+    op("g", [], ["IX"], lambda: g.iota(T.IX[:], [[1, 160]], 0, 0, allow_small_or_imprecise_dtypes=True))
+    op("g", [], ["CX"], lambda: g.iota(T.CX[:], [[16, 48]], WDUMMY - KEYADD, 0, allow_small_or_imprecise_dtypes=True))
+    fill(["MT"], T.MT[:], 0.0)
+    act(["MT"], ["MK"], T.MK[:], T.MT[:, 0:H], ACT.Identity, bias=1.0)
+
+    def clear(w):
+        act(["MK"], ["W%da" % w], WN[w][:, 0:H], T.MK[:], ACT.Copy, scale=0.0)
+        act(["MK"], ["W%db" % w], WN[w][:, H:WREAD], T.MK[:, 0:WREAD - H], ACT.Copy, scale=0.0)
+
+    clear(0)
+    ts(["CI0"], ["CI1"], T.CI[:, 1:2], T.CI[:, 0:1], 15, ALU.bitwise_and)
+    ts(["CI0"], ["CI2"], T.CI[:, 2:3], T.CI[:, 0:1], 112, ALU.bitwise_and)
+    ts(["CI0"], ["CI3"], T.CI[:, 3:4], T.CI[:, 0:1], 15, ALU.bitwise_and, 1, ALU.logical_shift_right)
+    fill(["SM0", "SM1", "SM2", "SM3", "SM4", "SM5"], T.SM[:], 0.0)
+    fill(["ZR"], T.ZR[:], 0.0)
+    cp(["CI0", "CI1", "CI2", "CI3"], ["CF"], T.CF[:], T.CI[:])
+    kc, ic, gcol, hc = T.CF[:, 0:1], T.CF[:, 1:2], T.CF[:, 2:3], T.CF[:, 3:4]
+    names = "b16 od sg hb ta t1 g2 g4 g6 r0 r1 tz w1 w2 wa ba sa e6 x0 y0 hib lob".split()
+    C = {k: T.CC[:, j:j + 1] for j, k in enumerate(names)}
+
+    def col(k, rd, in0, s1, op0, s2=None, op1=None):
+        ts(["CF"] + rd, [k], C[k], in0, s1, op0, s2, op1)
+
+    fill(["ET0"], T.ET[:, 0:1], 0.0)
+    fill(["EH0"], T.EH[:, 0:1], 0.0)
+    col("b16", [], gcol, 16.0, ALU.add)
+    ts(["CF", "IX"], ["ID"], T.ID[:], T.IX[:, 0:128], kc, ALU.is_equal)
+    ts(["CF", "IX"], ["NI"], T.NI[:], T.IX[:, 0:128], kc, ALU.is_equal, -1.0, ALU.mult)
+    ts(["CF", "IX"], ["IF"], T.IF[:], T.IX[:, 0:128], kc, ALU.is_equal)
+
+    ts(["MC"], ["M2a"], T.M2[:, 0:192], T.MC[:], 4095 - 63, ALU.bitwise_and)
+    ts(["MC"], ["M2b"], T.M2[:, 192:384], T.MC[:], 63, ALU.bitwise_and)
+    ts(["MC"], ["M2c"], T.M2[:, 384:576], T.MC[:], 12, ALU.logical_shift_right, 4095 - 63, ALU.bitwise_and)
+    cp(["M2a", "M2b"], ["MDa"], T.MD[:, 0:384], T.M2[:, 0:384])
+    ts(["MC"], ["M2d"], T.M2[:, 576:768], T.MC[:], 12, ALU.logical_shift_right, 63, ALU.bitwise_and)
+    cp(["TD"], ["TLt0", "TLh0"], T.TL0[:, 0:96], T.TD[:])
+    cp(["M2c", "M2d"], ["MDb"], T.MD[:, 384:768], T.M2[:, 384:768])
+    dmas("y", "dmt", ["MDa"], ["MT"], [(T.MT[i:128:16, :], T.MD[:, 192 * i:192 * i + 192]) for i in (0, 1)])
+    dmas("y", "dmt", ["MDb"], ["MTb"], [(T.MT[i:128:16, :], T.MD[:, 192 * i:192 * i + 192]) for i in (2, 3)])
+    writer["MT"] = writer["MTb"]
+    dmas("y", "dpc", [], ["PC"], [(T.PC[:], T.pre[:])])
+
+    def piece(b, j):
+        return b[:, 128 * j:128 * j + 128]
+
+    def row(i):
+        return T.ST[:, i:MH:16]
+
+    ts(["KC"], ["K2a"], T.K2[:, 0:128], T.KC[:], 4095, ALU.bitwise_and)
+    ts(["KC"], ["K2b"], T.K2[:, 128:256], T.KC[:], 12, ALU.logical_shift_right)
+    ts(["CF", "IX"], ["TG0"], T.TG0[:], T.IX[:, 0:8], hc, ALU.subtract, 1000.0, ALU.mult)
+    ts(["K2a", "K2b"], ["UF"], T.UF[:], T.K2[:], -1.0 / 64, ALU.mult, EMPTY / 64.0, ALU.add)
+    mm(["UF", "IF"], ["pd0"], *[[(piece(T.pd0, j), piece(T.UF, j), T.IF[:])] for j in range(2)])
+    ts(["TG0", "b16"], ["TG"], T.TG[:], T.TG0[:], C["b16"], ALU.add)
+    fill(["ST14"], row(14), 0.0)
+    fill(["ST15"], row(15), 0.0)
+    ts(["TG", "IX"], ["ZM0"], T.ZM0[:], T.IX[:, 0:144], T.TG[:, 0:1], ALU.is_equal)
+    ts(["TG", "IX"], ["ZM1"], T.ZM1[:], T.IX[:, 0:144], T.TG[:, 1:2], ALU.is_equal)
+    fill(["MK"], T.MK[:, 0:H:CH], 0.0)
+    ts(["b16", "IX"], ["ZO"], T.ZO[:], T.IX[:, 0:144], C["b16"], ALU.is_equal)
+    fill(["THa"], T.TH[:, 0:64], -16.0)
+    fill(["THb"], T.TH[:, 64:96], 0.0)
+    for r in range(RO):
+        fill(["LBx%d" % r], LB[r][:, 16:17], 0.0)
+    ts(["pd0"], ["DGh"], T.DG[:, 0:256], T.pd0[:, 0:256], RND, ALU.add, RND, ALU.subtract)
+    ts(["pd0"], ["pd1"], T.pd1[:, 0:256], T.pd0[:, 0:256], 0.0, ALU.is_gt)
+    ts(["pd0"], ["ZS"], T.ZS[:], T.pd0[:, 0:256], 0.0, ALU.is_gt)
+    tt(["pd0", "DGh"], ["DGl"], T.DG[:, 256:512], T.DG[:, 0:256], T.pd0[:, 0:256], ALU.subtract)
+    tt(["pd1", "ZS"], ["ST12"], row(12), piece(T.pd1, 0), piece(T.ZS, 1), ALU.add)
+    tt(["pd1", "ZS"], ["ST13"], row(13), piece(T.pd1, 0), piece(T.ZS, 1), ALU.max)
+    for i, z, d in ((0, 1, 0), (6, 0, 1), (1, 1, 2), (7, 0, 3)):
+        tt(["pd1", "DGh", "DGl"], ["ST%d" % i], row(i), piece(T.pd1, z), piece(T.DG, d), ALU.mult)
+
+    def both(o, j, i):
+        return [(o, T.ID[:], piece(T.DG, j)), (o, T.ID[:], piece(T.DG, j + 1)), (o, T.NI[:], row(i))]
+
+    def plus(o, i):
+        return [(o, T.ID[:], row(i))]
+
+    kk = ["DGh", "DGl", "ST0", "ST1", "ST6", "ST7", "ST13", "ID", "NI"]
+    mm(kk, ["pd2"], *[both(piece(T.pd2, j), d, i) for j, (d, i) in enumerate(((0, 0), (2, 1), (0, 6), (2, 7)))])
+    mm(kk, ["px"], *([plus(piece(T.px, j), j) + plus(piece(T.px, j), 13) for j in range(2)]
+                     + [both(piece(T.px, 2 + j), 2 * j, j) + plus(piece(T.px, 2 + j), 13) for j in range(2)]))
+    TB = ((T.pz, "pz", "v"), (T.pd0, "pd0", "s"), (T.pd1, "pd1", "v"), (T.pd2, "pd2", "s"))
+
+    def kid_rows():
+        for j in range(4):
+            act(["pd2"], ["ST%d" % (2 + j)], row(2 + j), piece(T.pd2, j), ACT.Copy)
+        for j in range(4):
+            act(["px"], ["ST%d" % (8 + j)], row(8 + j), piece(T.px, j), ACT.Copy)
+
+    def kid_table():
+        for b, (bank, bk, q) in enumerate(TB):
+            mm(["ST%d" % i for i in range(16)] + ["ID"], [bk], *[[(piece(bank, j), piece(T.ST, 4 * b + j), T.ID[:])] for j in range(4)])
+        for b, (bank, bk, q) in enumerate(TB):
+            copy(q, [bk], ["TT%d" % b], T.TT[:, MH * half + 512 * b:MH * half + 512 * b + 512], bank[:])
+        send(["TT%d" % b for b in range(4)], T.TT[:, mine], [(mate, T.TT[:, mine])], "ttx", whole)
+
+    col("od", [], hc, -2.0, ALU.mult, ic, ALU.add)
+    col("hb", [], hc, gcol, ALU.add, 8.0, ALU.add)
+    col("t1", [], ic, 4.0, ALU.is_lt)
+    col("g2", [], hc, 2.0, ALU.is_ge)
+    col("g4", [], hc, 4.0, ALU.is_ge)
+    col("g6", [], hc, 6.0, ALU.is_ge)
+    col("wa", [], ic, -2.0, ALU.mult, 25.0, ALU.add)
+    col("ta", ["od", "hb"], C["od"], 1000.0, ALU.mult, C["hb"], ALU.add)
+    col("ba", ["g2", "g4"], C["g2"], C["g4"], ALU.subtract)
+    col("y0", ["g4", "g6"], C["g4"], C["g6"], ALU.subtract, 0.5, ALU.mult)
+
+    def constants_pairs():
+        ts(["CF", "IX"], ["TI0"], T.TI0[:], T.IX[:, 12:14], ic, ALU.subtract, 1000.0, ALU.mult)
+        col("e6", ["ba"], hc, 6.0, ALU.is_equal, C["ba"], ALU.add)
+        ts(["ta", "IX"], ["PA"], T.PA[:], T.IX[:, 0:136], C["ta"], ALU.is_equal)
+        ts(["ta", "IX"], ["PB"], T.PB[:], T.IX[:, 0:136], 1000.0, ALU.add, C["ta"], ALU.is_equal)
+        ts(["TI0", "b16"], ["TI"], T.TI[:], T.TI0[:], C["b16"], ALU.add)
+        col("x0", ["e6", "t1"], C["e6"], 10000.0, ALU.mult, C["t1"], ALU.add)
+        col("sa", ["ba"], ic, 13.0, ALU.is_lt, C["ba"], ALU.subtract)
+        col("lob", ["ba", "t1"], C["ba"], -10000.0, ALU.mult, C["t1"], ALU.add)
+        ts(["TG", "wa", "IX"], ["ZA"], T.ZA[:], T.IX[:, 0:144], T.TG[:, 6:7], ALU.is_equal, C["wa"], ALU.mult)
+        ts(["TI", "IX"], ["ZB"], T.ZB[:], T.IX[:, 1:145], T.TI[:, 1:2], ALU.is_equal)
+        ts(["TI", "IX"], ["ZE"], T.ZE[:], T.IX[:, 0:144], T.TI[:, 0:1], ALU.is_equal, -8192.0, ALU.mult)
+        col("hib", ["x0", "y0"], C["x0"], C["y0"], ALU.add)
+        fill(["GA0"], T.GA[:, NP:NP + 1], 0.0)
+        fill(["GB0"], T.GB[:, 0:1], 0.0)
+        tt(["ZA", "ZB"], ["ZC"], T.ZC[:], T.ZA[:], T.ZB[:], ALU.add)
+        ts(["CF", "CX"], ["CD"], T.CD[:], T.CX[:], ic, ALU.add)
+
+    def constants_row():
+        col("sg", ["od"], C["od"], -2.0, ALU.mult, 1.0, ALU.add)
+        col("r0", ["g4", "g2"], C["g4"], -3.0, ALU.mult, C["g2"], ALU.subtract)
+        col("r1", ["g6", "b16"], C["g6"], 1000.0, ALU.mult, C["b16"], ALU.add)
+        col("w2", ["sg", "g4"], C["sg"], C["g4"], ALU.mult, 2.0, ALU.mult)
+        col("tz", ["r0", "r1"], C["r0"], hc, ALU.add, C["r1"], ALU.add)
+        fill(["Z1a"], T.Z1[:, 0:1], 0.0)
+        col("w1", ["w2", "sg"], C["w2"], -1.5, ALU.mult, C["sg"], ALU.add)
+        ts(["tz", "w2", "IX"], ["Z2"], T.Z2[:], T.IX[:, 0:148], C["tz"], ALU.is_equal, C["w2"], ALU.mult)
+        ts(["tz", "w1", "IX"], ["Z1"], T.Z1[:, 1:148], T.IX[:, 0:147], C["tz"], ALU.is_equal, C["w1"], ALU.mult)
+        tt(["Z1", "Z1a", "Z2"], ["ZT"], T.ZT[:], T.Z1[:], T.Z2[:], ALU.add)
+        for n, q in enumerate((13, 14, 15)):
+            op("g", ["ZT"], ["LTa%d" % q],
+               lambda: g.affine_select(piece(T.LT, 2 * n), T.ZT[:, 16 - q:144 - q], [[0, 8], [1, 16]], ALU.is_ge, 0.0, -8, 0))
+            op("g", ["ZT"], ["LTb%d" % q],
+               lambda: g.affine_select(piece(T.LT, 2 * n + 1), T.ZT[:, 32 - q:160 - q], [[0, 8], [-1, 16]], ALU.is_gt, 0.0, 8, 0))
+
+    def sel(z, q):
+        return z[:, 16 - q:144 - q]
+
+    def part_of(part):
+        return (0, 32) if part == "t" else (32, 64)
+
+    def gather_methods(q, tl, key, wr, lo, n):
+        copy(q, [key, "MT"], [wr], T.MG[:, 16 * lo:16 * (lo + n)], T.MT[:, :].indirect(tl[:, lo:lo + n]))
+
+    def method_list(part, j, rd, bank, bk):
+        lo, n = part_of(part)
+        z, zk = ((T.ZM0, "ZM0"), (T.ZM1, "ZM1"))[j]
+        mm(rd + [zk], [bk], [(bank[:, 0:n], sel(z, q), T.MG[:, 16 * lo + q:16 * (lo + n):16]) for q in range(16)])
+
+    def method_offsets(part, j, bank, bk):
+        lo, n = part_of(part)
+        cp([bk], ["MU%d%s" % (j, part)], T.MU[:, 96 * j + lo:96 * j + lo + n], bank[:, 0:n])
+
+    def scan(part):
+        e, a, n = (T.ET, 0, A) if part == "t" else (T.EH, A, H)
+        op("v", ["E" + part, "ET0", "EH0", "MK"], ["SR" + part],
+           lambda: g.vector.tensor_tensor_scan(T.SR[:, a:a + n], e[:, 0:n], T.MK[:, 0:n], 0.0, ALU.add, ALU.mult))
+
+    def diff0(part):
+        lo, n = part_of(part)
+        a, b = 16 * lo, 16 * (lo + n)
+        tt(["MU0" + part, "PC", "SR" + part], ["D0" + part], T.D0[:, a:b], T.PC[:, :].indirect(T.MU[:, lo:lo + n]), T.SR[:, a:b], ALU.subtract)
+
+    def cond1(part):
+        lo, n = part_of(part)
+        act(["MU1" + part, "PC"], ["P1" + part], T.P1[:, 16 * lo:16 * (lo + n)], T.PC[:, :].indirect(T.MU[:, 96 + lo:96 + lo + n]), ACT.Copy)
+
+    def diff1(part):
+        for k in ((0,) if part == "t" else (1, 2)):
+            c = slice(512 * k, 512 * k + 512)
+            mm(["SR" + part, "NI"], ["pd%d" % k], [(PD[k][:], T.NI[:], T.SR[:, c])], last=False)
+            mm(["P1" + part, "ID"], ["pd%d" % k], [(PD[k][:], T.ID[:], T.P1[:, c])], first=False)
+
+    def row_list(rnd, part):
+        lo, n, bank, bk = (0, 64, T.pz, "pz") if part == "h" else (64, 32, T.pmt, "pmt")
+        win, items = WN[rnd % 2], []
+        for q in range(16):
+            items.append((bank[:, 0:n], sel(T.ZT, q) if q < 13 else piece(T.LT, 2 * (q - 13)), win[:, 16 * (lo + 1) + q:16 * (lo + n + 1):16]))
+        for q in (13, 14, 15):
+            items.append((bank[:, 0:n], piece(T.LT, 2 * (q - 13) + 1), win[:, 16 * lo + q:16 * (lo + n):16]))
+        mm(["W%da" % (rnd % 2), "W%db" % (rnd % 2), "ZT"] + ["LT%s%d" % (x, q) for x in "ab" for q in (13, 14, 15)], [bk], items)
+
+    def row_types(rnd, part):
+        lo, n, bank, bk = (0, 64, T.pz, "pz") if part == "h" else (64, 32, T.pmt, "pmt")
+        key = "TL%s%d" % (part, rnd + 1)
+        ts([bk], [key], TL[rnd + 1][:, 32 + lo:32 + lo + n], bank[:, 0:n], -64.0, ALU.mult, float(EMPTY), ALU.add)
+        if part == "o":
+            send([key], TL[rnd + 1][:, 96:128], [((rank + 1) % N, TL[rnd + 1][:, 0:32])], "tail%d" % (rnd + 1))
+
+    lastrank = rank == N - 1
+    for rnd in range(RO):
+        tl, lb, win = TL[rnd], LB[rnd], WN[rnd % 2]
+        kt, kh, ko = "TLt%d" % rnd, "TLh%d" % rnd, "TLo%d" % rnd
+        st, sh = "SM%d" % (2 * rnd), "SM%d" % (2 * rnd + 1)
+        sumt, sumh = T.SM[:, 2 * rnd:2 * rnd + 1], T.SM[:, 2 * rnd + 1:2 * rnd + 2]
+        dsts = []
+        for d in range(N):
+            s = sum_senders(rnd, d)
+            if rank in s:
+                c = 16 - 2 * len(s) + 2 * s.index(rank)
+                dsts.append((d, lb[:, c:c + 2]))
+
+        def effects(q, key, wr, out, lo, n, sk=None, acc=None):
+            kw = {"accum_out": acc} if sk else {}
+            copy(q, [key, "EF"], [wr] + ([sk] if sk else []), out, T.EF[:, :].indirect(tl[:, lo:lo + n]), **kw)
+
+        gather_methods("v", tl, kh, "MGa", 32, 32)
+        if rnd > 0:
+            row_types(rnd - 1, "o")
+        effects("s", kh, "Eh", T.EH[:, 1:H + 1], 32, 64, None if lastrank else sh, sumh)
+        if rnd == 0:
+            effects("s", kt, "Et", T.ET[:, 1:A + 1], 0, 32, None if lastrank else st, sumt)
+        elif rank != N - 2:
+            effects("s", ko, "EJ", T.EJ[:], 96, 32, st, sumt)
+        send([st, sh], T.SM[:, 2 * rnd:2 * rnd + 2], dsts, "sum%d" % rnd)
+        if rnd == 0:
+            kid_rows()
+            gather_methods("s", tl, kt, "MGt", 0, 32)
+        gather_methods("v", tl, kh, "MGb", 64, 32)
+        method_list("h", 1, ["MGa", "MGb"], T.py, "py")
+        method_list("h", 0, ["MGa", "MGb"], T.pmh, "pmh")
+        scan("h")
+        method_offsets("h", 1, T.py, "py")
+        if rnd == 0:
+            method_offsets("h", 0, T.pmh, "pmh")
+            kid_table()
+            cond1("h")
+        else:
+            cond1("h")
+            method_offsets("h", 0, T.pmh, "pmh")
+            gather_methods("s", tl, kt, "MGt", 0, 32)
+            diff1("h")
+        method_list("t", 1, ["MGt"], T.py, "py")
+        method_list("t", 0, ["MGt"], T.pmt, "pmt")
+        if rnd == 0:
+            method_offsets("t", 1, T.py, "py")
+            diff1("h")
+        diff0("h")
+        if rnd > 0:
+            effects("v", kt, "Et", T.ET[:, 1:A + 1], 0, 32)
+        tt(["SRh", "Eh"], ["CTh"], lb[:, 21:28], T.SR[:, A + CH - 1:V - 1:CH], T.EH[:, CH:H:CH], ALU.add)
+        if rnd > 0:
+            method_offsets("t", 1, T.py, "py")
+        cond1("t")
+        scan("t")
+        method_offsets("t", 0, T.pmt, "pmt")
+        diff1("t")
+        diff0("t")
+        tt(["SRt", "Et"], ["CTt"], lb[:, 17:21], T.SR[:, CH - 1:A:CH], T.ET[:, CH:A + 1:CH], ALU.add)
+        ts(["MU0t", "MU0h"], ["pmh"], T.pmh[:, 96:192], T.MU[:, 0:96], -2048.0, ALU.add)
+        if lastrank and rnd > 0:
+            cp([st], ["LBx%d" % rnd], lb[:, 16:17], sumt)
+
+        ns = len(sum_senders(rnd, rank))
+        c0 = 16 - 2 * ns + (1 if (rnd > 0 and ns) else 0)
+        op("v", ["LBr%d" % rnd, "LBx%d" % rnd, "CTt", "CTh", "ZR"], ["BS"],
+           lambda: g.vector.tensor_tensor_scan(T.BS[:, c0:28], lb[:, c0:28], T.ZR[:, c0:28], 0.5, ALU.add, ALU.add))
+        ts(["MU1t", "MU1h"], ["MF"], T.MF[:], T.MU[:, 96:192], -2048.0, ALU.add)
+
+        def chunk(k):
+            return slice(CH * k, CH * k + CH), slice(CH * (k % 4), CH * (k % 4) + CH), T.BS[:, 16 + k:17 + k]
+
+        for k in (4, 5, 6, 7, 0, 1, 2, 3):
+            c, p, b = chunk(k)
+            act(["BS", "pd%d" % (k // 4)], ["B1%d" % k], T.B1[:, c], PD[k // 4][:, p], ACT.Sign, bias=b, scale=-1.0)
+        for k in range(NCH):
+            c, p, b = chunk(k)
+            ts(["BS", "D0t", "D0h"], ["B0%d" % k], T.B0[:, c], T.D0[:, c], b, ALU.is_le, -2.0, ALU.mult)
+        for k in range(8, NCH):
+            c, p, b = chunk(k)
+            ts(["BS", "pd2"], ["B1%d" % k], T.B1[:, c], PD[2][:, p], b, ALU.is_le, 2.0, ALU.mult)
+        mm(["B0%d" % k for k in range(NCH)] + ["ZO"], ["px"], [(T.px[:, 0:96], sel(T.ZO, q), T.B0[:, q:V:16]) for q in range(16)], last=False)
+        mm(["B1%d" % k for k in range(NCH)], ["px"], [(T.px[:, 0:96], sel(T.ZO, q), T.B1[:, q:V:16]) for q in range(16)], first=False)
+        tt(["MF", "pmh"], ["DM"], T.pmh[:, 0:96], T.MF[:], T.pmh[:, 96:192], ALU.subtract)
+        if rnd == 0:
+            constants_pairs()
+        if rnd == RO - 1:
+            ts(["BS"], ["BX"], T.BX[:, 0:NCH], T.BS[:, 16:28], -0.5, ALU.add)
+
+        tt(["px", "THa", "THb"], ["VT"], T.VT[:], T.px[:, 0:96], T.TH[:], ALU.is_gt)
+        tt(["VT", "DM", "pmh"], ["VD"], T.VD[:], T.VT[:], T.pmh[:, 0:96], ALU.mult)
+        tt(["VD", "pmh"], ["MS"], T.MS[:], T.VD[:], T.pmh[:, 96:192], ALU.add)
+        mm(["MS", "PA", "PB"], ["py"], *[[(T.py[:, 48 * j:48 * j + 48], z[:, 8:136], T.MS[:, 0:96:2]),
+                                          (T.py[:, 48 * j:48 * j + 48], z[:, 0:128], T.MS[:, 1:96:2])] for j, z in enumerate((T.PA, T.PB))])
+        ts(["py"], ["AB"], T.AB[:], T.py[:, 0:96], 2048.0, ALU.add)
+        tk = ["AB", "TTx"] + ["TT%d" % b for b in range(4)]
+        act(tk + ["sa", "ba"], ["GA"], T.GA[:, 0:NP], T.TT[:, :].indirect(T.AB[:, 0:48]), ACT.Identity, scale=C["sa"], bias=C["ba"])
+        ts(tk + ["hib", "lob"], ["GB"], T.GB[:, 1:NP + 1], T.TT[:, :].indirect(T.AB[:, 48:96]), C["hib"], ALU.min, C["lob"], ALU.max)
+        if rnd == RO - 1:
+            for k in range(3):
+                c = slice(512 * k, 512 * k + 512)
+                mm(["SRt", "SRh", "ID"], ["pd%d" % k], [(PD[k][:], T.ID[:], T.SR[:, c])])
+                for j in range(4 * k, 4 * k + 4):
+                    cc, p, _ = chunk(j)
+                    act(["BX", "pd%d" % k], ["YS%d" % j], T.YS[:, cc], PD[k][:, p], ACT.Identity, bias=T.BX[:, j:j + 1])
+                dmas("y", "dys%d" % k, ["YS%d" % j for j in range(4 * k, 4 * k + 4)], [], [(T.ys[:, c], T.YS[:, c])])
+
+        mm(["GB", "ZE"], ["px"], [(T.px[:, 0:48], sel(T.ZE, q), T.GB[:, 1 + q:NP + 1:16]) for q in range(16)], last=False)
+        op("v", ["GA", "GB", "GA0", "GB0"], ["KS"],
+           lambda: g.vector.tensor_tensor_scan(T.KS[:, 0:NP + 1], T.GA[:, 0:NP + 1], T.GB[:, 0:NP + 1], -float(KEY0), ALU.add, ALU.add))
+        mm(["GA"], ["px"], [(T.px[:, 0:48], sel(T.ZE, q), T.GA[:, q:NP:16]) for q in range(16)], first=False)
+        mm(["KS", "ZA", "ZB", "ZC"], ["py"],
+           [(T.py[:, 0:48], sel(T.ZA if q == 0 else T.ZB if q == 16 else T.ZC, q), T.KS[:, q:q + NP - 15:16]) for q in range(17)])
+        if rnd == 0:
+            constants_row()
+        tt(["px", "CD"], ["CE"], T.CE[:], T.px[:, 0:48], T.CD[:], ALU.add)
+        tt(["py", "CE"], ["OF"], T.OF[:], T.py[:, 0:48], T.CE[:], ALU.max)
+        ts(["OF"], ["OU"], T.OU[:], T.OF[:], float(KEYADD), ALU.add)
+        tt(["OU", "GA", "GB"], ["W%da" % (rnd % 2), "W%db" % (rnd % 2)], win[:, :].indirect(T.OU[:]), T.GA[:, 0:NP], T.GB[:, 1:NP + 1], ALU.mult)
+
+        if rnd + 1 < RO:
+            clear((rnd + 1) % 2)
+            row_list(rnd, "h")
+            row_list(rnd, "o")
+            row_types(rnd, "h")
+        else:
+            row_list(rnd, "o")
+            row_list(rnd, "h")
+            row_types(rnd, "o")
+            row_types(rnd, "h")
+
+    dmas("y", "dyp", ["TLh%d" % RO, "TLt%d" % RO], [], [(T.yp[:], T.YP[:, 0:96])])
+    wait("y", list(count.items()))

@@ -9,6 +9,7 @@ EMPTY = W - 1
 CH = 128
 NCH = V // CH
 NP = V // 2
+GBO = NP + 16
 WREAD = V + 16
 WDUMMY = 2 * V + 16
 WCOLS = WDUMMY + NP
@@ -22,11 +23,11 @@ SCRATCH = {k: ("sbuf", [128, n], d) for d, names in (
     (I32, dict(TD=96, KC=128, K2=256, MC=192, M2=768, CI=4)),
     (BF, dict(MD=768, DG=512, ST=MH, ZS=256, EF=W, PC=M, MT=W, TT=M, IX=160,
               ZO=144, ZM0=144, ZM1=144, Z1=148, Z2=148, ZT=148, LT=768, ZA=144, ZB=144, ZC=144, ZE=144, PA=136, PB=136,
-              ID=128, NI=128, MK=H, ET=A + 2, EH=H + 2, EJ=A, MG=V, P1=V, B0=V, B1=V, GA=NP + 2, GB=NP + 2,
+              ID=128, NI=128, MK=H, ET=A + 2, EH=H + 2, EJ=A, MG=V, P1=V, B0=V, B1=V, G2=GBO + NP,
               W0=WCOLS, W1=WCOLS)),
-    (F32, dict(CF=4, CX=48, CD=48, CC=32, TG=8, TG0=8, TI=2, TI0=2, ZR=32, TH=96, YP=128, YS=V, MF=96, VT=96, VD=96,
-               CE=48, OF=48, SM=8, LB0=32, LB1=32, LB2=32, BS=32, BX=16, UF=256, IF=128)),
-    (F16, dict(SR=V, D0=V, MS=96, KS=NP + 2)),
+    (F32, dict(CF=4, CX=48, CD=48, CC=32, TG=8, TG0=8, TI=2, TI0=2, ZR=32, TH=96, YP=128, YS=V, MF=96, VT=192,
+               CE=48, CE0=48, OF=48, SM=8, LB0=32, LB1=32, LB2=32, BS=32, BX=16, UF=256, IF=128)),
+    (F16, dict(SR=V, D0=V, MS=192, KS=NP + 2)),
     (U16, dict(TL0=128, TL1=128, TL2=128, MU=192, AB=96, OU=48)),
 ) for k, n in names.items()}
 PSUM_KEYS = ("pd0", "pd1", "pd2", "pmh", "pmt", "px", "py", "pz")
@@ -292,60 +293,65 @@ def rank_program(g, core, T, topo):
     col("wa", [], ic, -2.0, ALU.mult, 25.0, ALU.add)
     col("ta", ["od", "hb"], C["od"], 1000.0, ALU.mult, C["hb"], ALU.add)
     col("ba", ["g2", "g4"], C["g2"], C["g4"], ALU.subtract)
-    col("y0", ["g4", "g6"], C["g4"], C["g6"], ALU.subtract, 0.5, ALU.mult)
+    fill(["VT"], T.VT[:], 0.0)
 
-    def constants_pairs():
+    def late_constants():
+        col("sg", ["od"], C["od"], -2.0, ALU.mult, 1.0, ALU.add)
+        col("r0", ["g4", "g2"], C["g4"], -3.0, ALU.mult, C["g2"], ALU.subtract)
+        col("r1", ["g6", "b16"], C["g6"], 1000.0, ALU.mult, C["b16"], ALU.add)
         ts(["CF", "IX"], ["TI0"], T.TI0[:], T.IX[:, 12:14], ic, ALU.subtract, 1000.0, ALU.mult)
+        col("w2", ["sg", "g4"], C["sg"], C["g4"], ALU.mult, 2.0, ALU.mult)
+        col("tz", ["r0", "r1"], C["r0"], hc, ALU.add, C["r1"], ALU.add)
         col("e6", ["ba"], hc, 6.0, ALU.is_equal, C["ba"], ALU.add)
+        col("y0", ["g4", "g6"], C["g4"], C["g6"], ALU.subtract, 0.5, ALU.mult)
+        col("w1", ["w2", "sg"], C["w2"], -1.5, ALU.mult, C["sg"], ALU.add)
         ts(["ta", "IX"], ["PA"], T.PA[:], T.IX[:, 0:136], C["ta"], ALU.is_equal)
         ts(["ta", "IX"], ["PB"], T.PB[:], T.IX[:, 0:136], 1000.0, ALU.add, C["ta"], ALU.is_equal)
         ts(["TI0", "b16"], ["TI"], T.TI[:], T.TI0[:], C["b16"], ALU.add)
         col("x0", ["e6", "t1"], C["e6"], 10000.0, ALU.mult, C["t1"], ALU.add)
         col("sa", ["ba"], ic, 13.0, ALU.is_lt, C["ba"], ALU.subtract)
         col("lob", ["ba", "t1"], C["ba"], -10000.0, ALU.mult, C["t1"], ALU.add)
-        ts(["TG", "wa", "IX"], ["ZA"], T.ZA[:], T.IX[:, 0:144], T.TG[:, 6:7], ALU.is_equal, C["wa"], ALU.mult)
-        ts(["TI", "IX"], ["ZB"], T.ZB[:], T.IX[:, 1:145], T.TI[:, 1:2], ALU.is_equal)
-        ts(["TI", "IX"], ["ZE"], T.ZE[:], T.IX[:, 0:144], T.TI[:, 0:1], ALU.is_equal, -8192.0, ALU.mult)
-        col("hib", ["x0", "y0"], C["x0"], C["y0"], ALU.add)
-        fill(["GA0"], T.GA[:, NP:NP + 1], 0.0)
-        fill(["GB0"], T.GB[:, 0:1], 0.0)
-        tt(["ZA", "ZB"], ["ZC"], T.ZC[:], T.ZA[:], T.ZB[:], ALU.add)
-        ts(["CF", "CX"], ["CD"], T.CD[:], T.CX[:], ic, ALU.add)
-
-    def constants_row():
-        col("sg", ["od"], C["od"], -2.0, ALU.mult, 1.0, ALU.add)
-        col("r0", ["g4", "g2"], C["g4"], -3.0, ALU.mult, C["g2"], ALU.subtract)
-        col("r1", ["g6", "b16"], C["g6"], 1000.0, ALU.mult, C["b16"], ALU.add)
-        col("w2", ["sg", "g4"], C["sg"], C["g4"], ALU.mult, 2.0, ALU.mult)
-        col("tz", ["r0", "r1"], C["r0"], hc, ALU.add, C["r1"], ALU.add)
         fill(["Z1a"], T.Z1[:, 0:1], 0.0)
-        col("w1", ["w2", "sg"], C["w2"], -1.5, ALU.mult, C["sg"], ALU.add)
         ts(["tz", "w2", "IX"], ["Z2"], T.Z2[:], T.IX[:, 0:148], C["tz"], ALU.is_equal, C["w2"], ALU.mult)
         ts(["tz", "w1", "IX"], ["Z1"], T.Z1[:, 1:148], T.IX[:, 0:147], C["tz"], ALU.is_equal, C["w1"], ALU.mult)
-        tt(["Z1", "Z1a", "Z2"], ["ZT"], T.ZT[:], T.Z1[:], T.Z2[:], ALU.add)
-        for n, q in enumerate((13, 14, 15)):
-            op("g", ["ZT"], ["LTa%d" % q],
-               lambda: g.affine_select(piece(T.LT, 2 * n), T.ZT[:, 16 - q:144 - q], [[0, 8], [1, 16]], ALU.is_ge, 0.0, -8, 0))
-            op("g", ["ZT"], ["LTb%d" % q],
-               lambda: g.affine_select(piece(T.LT, 2 * n + 1), T.ZT[:, 32 - q:160 - q], [[0, 8], [-1, 16]], ALU.is_gt, 0.0, 8, 0))
+        col("hib", ["x0", "y0"], C["x0"], C["y0"], ALU.add)
+        fill(["G0"], T.G2[:, NP:GBO], 0.0)
+
+    def selectors(step):
+        if step == 0:
+            ts(["TG", "wa", "IX"], ["ZA"], T.ZA[:], T.IX[:, 0:144], T.TG[:, 6:7], ALU.is_equal, C["wa"], ALU.mult)
+            ts(["TI", "IX"], ["ZB"], T.ZB[:], T.IX[:, 1:145], T.TI[:, 1:2], ALU.is_equal)
+        elif step == 1:
+            ts(["TI", "IX"], ["ZE"], T.ZE[:], T.IX[:, 0:144], T.TI[:, 0:1], ALU.is_equal, -8192.0, ALU.mult)
+            tt(["ZA", "ZB"], ["ZC"], T.ZC[:], T.ZA[:], T.ZB[:], ALU.add)
+        else:
+            tt(["Z1", "Z1a", "Z2"], ["ZT"], T.ZT[:], T.Z1[:], T.Z2[:], ALU.add)
+            ts(["CF", "CX"], ["CD"], T.CD[:], T.CX[:], ic, ALU.add)
+            for n, q in enumerate((13, 14, 15)):
+                op("g", ["ZT"], ["LTa%d" % q],
+                   lambda: g.affine_select(piece(T.LT, 2 * n), T.ZT[:, 16 - q:144 - q], [[0, 8], [1, 16]], ALU.is_ge, 0.0, -8, 0))
+                op("g", ["ZT"], ["LTb%d" % q],
+                   lambda: g.affine_select(piece(T.LT, 2 * n + 1), T.ZT[:, 32 - q:160 - q], [[0, 8], [-1, 16]], ALU.is_gt, 0.0, 8, 0))
 
     def sel(z, q):
         return z[:, 16 - q:144 - q]
 
     def part_of(part):
-        return (0, 32) if part == "t" else (32, 64)
+        lo = 32 * "tab".index(part)
+        return lo, slice(16 * lo, 16 * lo + A), "SRt" if part == "t" else "SRh"
 
-    def gather_methods(q, tl, key, wr, lo, n):
-        copy(q, [key, "MT"], [wr], T.MG[:, 16 * lo:16 * (lo + n)], T.MT[:, :].indirect(tl[:, lo:lo + n]))
+    def gather_methods(q, tl, key, part):
+        lo, c, _ = part_of(part)
+        copy(q, [key, "MT"], ["MG" + part], T.MG[:, c], T.MT[:, :].indirect(tl[:, lo:lo + 32]))
 
-    def method_list(part, j, rd, bank, bk):
-        lo, n = part_of(part)
+    def method_list(part, j, bk):
+        lo = part_of(part)[0]
         z, zk = ((T.ZM0, "ZM0"), (T.ZM1, "ZM1"))[j]
-        mm(rd + [zk], [bk], [(bank[:, 0:n], sel(z, q), T.MG[:, 16 * lo + q:16 * (lo + n):16]) for q in range(16)])
+        mm(["MG" + part, zk], [bk], [(T[bk][:, 0:32], sel(z, q), T.MG[:, 16 * lo + q:16 * lo + A:16]) for q in range(16)])
 
-    def method_offsets(part, j, bank, bk):
-        lo, n = part_of(part)
-        cp([bk], ["MU%d%s" % (j, part)], T.MU[:, 96 * j + lo:96 * j + lo + n], bank[:, 0:n])
+    def method_offsets(part, j, bk):
+        lo = part_of(part)[0]
+        cp([bk], ["MU%d%s" % (j, part)], T.MU[:, 96 * j + lo:96 * j + lo + 32], T[bk][:, 0:32])
 
     def scan(part):
         e, a, n = (T.ET, 0, A) if part == "t" else (T.EH, A, H)
@@ -353,19 +359,17 @@ def rank_program(g, core, T, topo):
            lambda: g.vector.tensor_tensor_scan(T.SR[:, a:a + n], e[:, 0:n], T.MK[:, 0:n], 0.0, ALU.add, ALU.mult))
 
     def diff0(part):
-        lo, n = part_of(part)
-        a, b = 16 * lo, 16 * (lo + n)
-        tt(["MU0" + part, "PC", "SR" + part], ["D0" + part], T.D0[:, a:b], T.PC[:, :].indirect(T.MU[:, lo:lo + n]), T.SR[:, a:b], ALU.subtract)
+        lo, c, sr = part_of(part)
+        tt(["MU0" + part, "PC", sr], ["D0" + part], T.D0[:, c], T.PC[:, :].indirect(T.MU[:, lo:lo + 32]), T.SR[:, c], ALU.subtract)
 
     def cond1(part):
-        lo, n = part_of(part)
-        act(["MU1" + part, "PC"], ["P1" + part], T.P1[:, 16 * lo:16 * (lo + n)], T.PC[:, :].indirect(T.MU[:, 96 + lo:96 + lo + n]), ACT.Copy)
+        lo, c, sr = part_of(part)
+        act(["MU1" + part, "PC"], ["P1" + part], T.P1[:, c], T.PC[:, :].indirect(T.MU[:, 96 + lo:96 + lo + 32]), ACT.Copy)
 
     def diff1(part):
-        for k in ((0,) if part == "t" else (1, 2)):
-            c = slice(512 * k, 512 * k + 512)
-            mm(["SR" + part, "NI"], ["pd%d" % k], [(PD[k][:], T.NI[:], T.SR[:, c])], last=False)
-            mm(["P1" + part, "ID"], ["pd%d" % k], [(PD[k][:], T.ID[:], T.P1[:, c])], first=False)
+        lo, c, sr = part_of(part)
+        k = lo // 32
+        mm([sr, "P1" + part, "NI", "ID"], ["pd%d" % k], [(PD[k][:], T.NI[:], T.SR[:, c]), (PD[k][:], T.ID[:], T.P1[:, c])])
 
     def row_list(rnd, part):
         lo, n, bank, bk = (0, 64, T.pz, "pz") if part == "h" else (64, 32, T.pmt, "pmt")
@@ -384,13 +388,14 @@ def rank_program(g, core, T, topo):
             send([key], TL[rnd + 1][:, 96:128], [((rank + 1) % N, TL[rnd + 1][:, 0:32])], "tail%d" % (rnd + 1))
 
     lastrank = rank == N - 1
+    GA, GB = T.G2[:, 0:NP], T.G2[:, GBO:GBO + NP]
     for rnd in range(RO):
         tl, lb, win = TL[rnd], LB[rnd], WN[rnd % 2]
         kt, kh, ko = "TLt%d" % rnd, "TLh%d" % rnd, "TLo%d" % rnd
         st, sh = "SM%d" % (2 * rnd), "SM%d" % (2 * rnd + 1)
         sumt, sumh = T.SM[:, 2 * rnd:2 * rnd + 1], T.SM[:, 2 * rnd + 1:2 * rnd + 2]
         dsts = []
-        for d in range(N):
+        for d in (range(N) if lastrank else range(N - 1, -1, -1)):
             s = sum_senders(rnd, d)
             if rank in s:
                 c = 16 - 2 * len(s) + 2 * s.index(rank)
@@ -400,7 +405,7 @@ def rank_program(g, core, T, topo):
             kw = {"accum_out": acc} if sk else {}
             copy(q, [key, "EF"], [wr] + ([sk] if sk else []), out, T.EF[:, :].indirect(tl[:, lo:lo + n]), **kw)
 
-        gather_methods("v", tl, kh, "MGa", 32, 32)
+        gather_methods("v", tl, kh, "a")
         if rnd > 0:
             row_types(rnd - 1, "o")
         effects("s", kh, "Eh", T.EH[:, 1:H + 1], 32, 64, None if lastrank else sh, sumh)
@@ -409,49 +414,53 @@ def rank_program(g, core, T, topo):
         elif rank != N - 2:
             effects("s", ko, "EJ", T.EJ[:], 96, 32, st, sumt)
         send([st, sh], T.SM[:, 2 * rnd:2 * rnd + 2], dsts, "sum%d" % rnd)
+        method_list("a", 0, "pmh")
+        method_list("a", 1, "py")
+        gather_methods("v", tl, kh, "b")
         if rnd == 0:
             kid_rows()
-            gather_methods("s", tl, kt, "MGt", 0, 32)
-        gather_methods("v", tl, kh, "MGb", 64, 32)
-        method_list("h", 1, ["MGa", "MGb"], T.py, "py")
-        method_list("h", 0, ["MGa", "MGb"], T.pmh, "pmh")
+            gather_methods("s", tl, kt, "t")
+        method_list("b", 0, "px")
+        method_list("b", 1, "pmt")
+        method_offsets("a", 0, "pmh")
+        method_offsets("a", 1, "py")
         scan("h")
-        method_offsets("h", 1, T.py, "py")
         if rnd == 0:
-            method_offsets("h", 0, T.pmh, "pmh")
+            method_offsets("b", 0, "px")
+            method_offsets("b", 1, "pmt")
             kid_table()
-            cond1("h")
+            cond1("a")
+            diff0("a")
         else:
-            cond1("h")
-            method_offsets("h", 0, T.pmh, "pmh")
-            gather_methods("s", tl, kt, "MGt", 0, 32)
-            diff1("h")
-        method_list("t", 1, ["MGt"], T.py, "py")
-        method_list("t", 0, ["MGt"], T.pmt, "pmt")
-        if rnd == 0:
-            method_offsets("t", 1, T.py, "py")
-            diff1("h")
-        diff0("h")
+            cond1("a")
+            diff0("a")
+            method_offsets("b", 0, "px")
+            method_offsets("b", 1, "pmt")
+            gather_methods("s", tl, kt, "t")
+        diff1("a")
+        method_list("t", 1, "py")
+        method_list("t", 0, "pmh")
+        cond1("b")
+        diff0("b")
         if rnd > 0:
             effects("v", kt, "Et", T.ET[:, 1:A + 1], 0, 32)
-        tt(["SRh", "Eh"], ["CTh"], lb[:, 21:28], T.SR[:, A + CH - 1:V - 1:CH], T.EH[:, CH:H:CH], ALU.add)
-        if rnd > 0:
-            method_offsets("t", 1, T.py, "py")
+        method_offsets("t", 1, "py")
         cond1("t")
+        diff1("b")
         scan("t")
-        method_offsets("t", 0, T.pmt, "pmt")
-        diff1("t")
-        diff0("t")
+        method_offsets("t", 0, "pmh")
+        tt(["SRh", "Eh"], ["CTh"], lb[:, 21:28], T.SR[:, A + CH - 1:V - 1:CH], T.EH[:, CH:H:CH], ALU.add)
         tt(["SRt", "Et"], ["CTt"], lb[:, 17:21], T.SR[:, CH - 1:A:CH], T.ET[:, CH:A + 1:CH], ALU.add)
-        ts(["MU0t", "MU0h"], ["pmh"], T.pmh[:, 96:192], T.MU[:, 0:96], -2048.0, ALU.add)
         if lastrank and rnd > 0:
             cp([st], ["LBx%d" % rnd], lb[:, 16:17], sumt)
+        diff1("t")
+        diff0("t")
 
         ns = len(sum_senders(rnd, rank))
         c0 = 16 - 2 * ns + (1 if (rnd > 0 and ns) else 0)
         op("v", ["LBr%d" % rnd, "LBx%d" % rnd, "CTt", "CTh", "ZR"], ["BS"],
            lambda: g.vector.tensor_tensor_scan(T.BS[:, c0:28], lb[:, c0:28], T.ZR[:, c0:28], 0.5, ALU.add, ALU.add))
-        ts(["MU1t", "MU1h"], ["MF"], T.MF[:], T.MU[:, 96:192], -2048.0, ALU.add)
+        ts(["MU1t", "MU1a", "MU1b"], ["MF"], T.MF[:], T.MU[:, 96:192], -2048.0, ALU.add)
 
         def chunk(k):
             return slice(CH * k, CH * k + CH), slice(CH * (k % 4), CH * (k % 4) + CH), T.BS[:, 16 + k:17 + k]
@@ -461,27 +470,32 @@ def rank_program(g, core, T, topo):
             act(["BS", "pd%d" % (k // 4)], ["B1%d" % k], T.B1[:, c], PD[k // 4][:, p], ACT.Sign, bias=b, scale=-1.0)
         for k in range(NCH):
             c, p, b = chunk(k)
-            ts(["BS", "D0t", "D0h"], ["B0%d" % k], T.B0[:, c], T.D0[:, c], b, ALU.is_le, -2.0, ALU.mult)
+            ts(["BS", "D0t", "D0a", "D0b"], ["B0%d" % k], T.B0[:, c], T.D0[:, c], b, ALU.is_le, -2.0, ALU.mult)
         for k in range(8, NCH):
             c, p, b = chunk(k)
             ts(["BS", "pd2"], ["B1%d" % k], T.B1[:, c], PD[2][:, p], b, ALU.is_le, 2.0, ALU.mult)
         mm(["B0%d" % k for k in range(NCH)] + ["ZO"], ["px"], [(T.px[:, 0:96], sel(T.ZO, q), T.B0[:, q:V:16]) for q in range(16)], last=False)
         mm(["B1%d" % k for k in range(NCH)], ["px"], [(T.px[:, 0:96], sel(T.ZO, q), T.B1[:, q:V:16]) for q in range(16)], first=False)
-        tt(["MF", "pmh"], ["DM"], T.pmh[:, 0:96], T.MF[:], T.pmh[:, 96:192], ALU.subtract)
-        if rnd == 0:
-            constants_pairs()
+        ts(["MU0t", "MU0a", "MU0b"], ["pmh"], T.pmh[:, 1:192:2], T.MU[:, 0:96], -2048.0, ALU.add)
         if rnd == RO - 1:
             ts(["BS"], ["BX"], T.BX[:, 0:NCH], T.BS[:, 16:28], -0.5, ALU.add)
+        if rnd == 0:
+            late_constants()
+        tt(["MF", "pmh"], ["DM"], T.pmh[:, 0:192:2], T.MF[:], T.pmh[:, 1:192:2], ALU.subtract)
 
-        tt(["px", "THa", "THb"], ["VT"], T.VT[:], T.px[:, 0:96], T.TH[:], ALU.is_gt)
-        tt(["VT", "DM", "pmh"], ["VD"], T.VD[:], T.VT[:], T.pmh[:, 0:96], ALU.mult)
-        tt(["VD", "pmh"], ["MS"], T.MS[:], T.VD[:], T.pmh[:, 96:192], ALU.add)
-        mm(["MS", "PA", "PB"], ["py"], *[[(T.py[:, 48 * j:48 * j + 48], z[:, 8:136], T.MS[:, 0:96:2]),
-                                          (T.py[:, 48 * j:48 * j + 48], z[:, 0:128], T.MS[:, 1:96:2])] for j, z in enumerate((T.PA, T.PB))])
+        tt(["px", "THa", "THb"], ["VT"], T.VT[:, 1:192:2], T.px[:, 0:96], T.TH[:], ALU.is_gt)
+        if rnd == 0:
+            selectors(0)
+        op("v", ["VT", "DM", "pmh"], ["MS"],
+           lambda: g.vector.tensor_tensor_scan(T.MS[:], T.VT[:], T.pmh[:, 0:192], 0.0, ALU.mult, ALU.add))
+        mm(["MS", "PA", "PB"], ["py"], *[[(T.py[:, 48 * j:48 * j + 48], z[:, 8:136], T.MS[:, 1:192:4]),
+                                          (T.py[:, 48 * j:48 * j + 48], z[:, 0:128], T.MS[:, 3:192:4])] for j, z in enumerate((T.PA, T.PB))])
+        if rnd == 0:
+            selectors(1)
         ts(["py"], ["AB"], T.AB[:], T.py[:, 0:96], 2048.0, ALU.add)
         tk = ["AB", "TTx"] + ["TT%d" % b for b in range(4)]
-        act(tk + ["sa", "ba"], ["GA"], T.GA[:, 0:NP], T.TT[:, :].indirect(T.AB[:, 0:48]), ACT.Identity, scale=C["sa"], bias=C["ba"])
-        ts(tk + ["hib", "lob"], ["GB"], T.GB[:, 1:NP + 1], T.TT[:, :].indirect(T.AB[:, 48:96]), C["hib"], ALU.min, C["lob"], ALU.max)
+        act(tk + ["sa", "ba"], ["GA"], GA, T.TT[:, :].indirect(T.AB[:, 0:48]), ACT.Identity, scale=C["sa"], bias=C["ba"])
+        ts(tk + ["hib", "lob"], ["GB"], GB, T.TT[:, :].indirect(T.AB[:, 48:96]), C["hib"], ALU.min, C["lob"], ALU.max)
         if rnd == RO - 1:
             for k in range(3):
                 c = slice(512 * k, 512 * k + 512)
@@ -491,18 +505,18 @@ def rank_program(g, core, T, topo):
                     act(["BX", "pd%d" % k], ["YS%d" % j], T.YS[:, cc], PD[k][:, p], ACT.Identity, bias=T.BX[:, j:j + 1])
                 dmas("y", "dys%d" % k, ["YS%d" % j for j in range(4 * k, 4 * k + 4)], [], [(T.ys[:, c], T.YS[:, c])])
 
-        mm(["GB", "ZE"], ["px"], [(T.px[:, 0:48], sel(T.ZE, q), T.GB[:, 1 + q:NP + 1:16]) for q in range(16)], last=False)
-        op("v", ["GA", "GB", "GA0", "GB0"], ["KS"],
-           lambda: g.vector.tensor_tensor_scan(T.KS[:, 0:NP + 1], T.GA[:, 0:NP + 1], T.GB[:, 0:NP + 1], -float(KEY0), ALU.add, ALU.add))
-        mm(["GA"], ["px"], [(T.px[:, 0:48], sel(T.ZE, q), T.GA[:, q:NP:16]) for q in range(16)], first=False)
+        mm(["GA", "GB", "G0", "ZE"], ["px"], [(T.px[:, 0:97], sel(T.ZE, q), T.G2[:, q:GBO + NP:16]) for q in range(16)])
+        op("v", ["GA", "GB", "G0"], ["KS"],
+           lambda: g.vector.tensor_tensor_scan(T.KS[:, 0:NP + 1], T.G2[:, 0:NP + 1], T.G2[:, GBO - 1:GBO + NP], -float(KEY0), ALU.add, ALU.add))
         mm(["KS", "ZA", "ZB", "ZC"], ["py"],
            [(T.py[:, 0:48], sel(T.ZA if q == 0 else T.ZB if q == 16 else T.ZC, q), T.KS[:, q:q + NP - 15:16]) for q in range(17)])
         if rnd == 0:
-            constants_row()
-        tt(["px", "CD"], ["CE"], T.CE[:], T.px[:, 0:48], T.CD[:], ALU.add)
+            selectors(2)
+        tt(["px", "CD"], ["CE0"], T.CE0[:], T.px[:, 0:48], T.CD[:], ALU.add)
+        tt(["px", "CE0"], ["CE"], T.CE[:], T.px[:, 49:97], T.CE0[:], ALU.add)
         tt(["py", "CE"], ["OF"], T.OF[:], T.py[:, 0:48], T.CE[:], ALU.max)
         ts(["OF"], ["OU"], T.OU[:], T.OF[:], float(KEYADD), ALU.add)
-        tt(["OU", "GA", "GB"], ["W%da" % (rnd % 2), "W%db" % (rnd % 2)], win[:, :].indirect(T.OU[:]), T.GA[:, 0:NP], T.GB[:, 1:NP + 1], ALU.mult)
+        tt(["OU", "GA", "GB"], ["W%da" % (rnd % 2), "W%db" % (rnd % 2)], win[:, :].indirect(T.OU[:]), GA, GB, ALU.mult)
 
         if rnd + 1 < RO:
             clear((rnd + 1) % 2)

@@ -6,8 +6,6 @@ ACT = ActivationFunctionType
 N, V, A, W, M, RO = 8, 1536, 512, 3072, 4096, 3
 H = V - A
 EMPTY = W - 1
-CH = 128
-NCH = V // CH
 NP = V // 2
 GBO = NP + 16
 WREAD = V + 16
@@ -16,41 +14,28 @@ WCOLS = WDUMMY + NP
 KEY0 = 1024
 KEYADD = KEY0 + 13
 RND = 12582912.0
-MH = M // 2
 F32, BF, F16, I32, U16 = "float32", "bfloat16", "float16", "int32", "uint16"
 
 SCRATCH = {k: ("sbuf", [128, n], d) for d, names in (
-    (I32, dict(TD=96, KC=128, K2=256, MC=192, M2=768, CI=4)),
-    (BF, dict(MD=768, DG=512, ST=MH, ZS=256, EF=W, PC=M, MT=W, TT=M, IX=160,
-              ZO=144, ZM0=144, ZM1=144, Z1=148, Z2=148, ZT=148, LT=768, ZA=144, ZB=144, ZC=144, ZE=144, PA=136, PB=136,
-              ID=128, NI=128, MK=H, ET=A + 2, EH=H + 2, EJ=A, MG=V, P1=V, B0=V, B1=V, G2=GBO + NP,
+    (I32, dict(TD=96, KC=128, K2=256, MC=96, M2=96, CI=4)),
+    (BF, dict(MD=96, DG=128, ST=512, ZS=64, O1=512, EF=W, EA=W, PC=M, MT=W, TT=M, IX=160, IM=128,
+              ZO=144, ZN=144, ZM0=144, ZM1=144, Z1=148, Z2=148, ZT=148, Y1=148, Y2=148, YT=148, LT=768, LY=768,
+              ZA=144, ZB=144, ZC=144, ZE=144, PA=136, PB=136,
+              ID=128, NI=128, ZW=V, EB=V + 2, EY=V + 2, MG=V, P1=V, B0=V, B1=V, SB=V, G2=GBO + NP,
               W0=WCOLS, W1=WCOLS)),
-    (F32, dict(CF=4, CX=48, CD=48, CC=32, TG=8, TG0=8, TI=2, TI0=2, ZR=32, TH=96, YP=128, YS=V, MF=96, VT=192,
-               CE=48, CE0=48, OF=48, SM=8, LB0=32, LB1=32, LB2=32, BS=32, BX=16, UF=256, IF=128)),
-    (F16, dict(SR=V, D0=V, MS=192, KS=NP + 2)),
-    (U16, dict(TL0=128, TL1=128, TL2=128, MU=192, AB=96, OU=48)),
+    (F32, dict(CF=4, CX=48, CD=48, CC=32, TG=8, TG0=8, TI=2, TI0=2, YP=96, YS=V, MF=96, VT=192,
+               CE=48, CE0=48, OF=48, SM=2, UF=256, IF=32, L1=128, LOW=128, XB=16, XR=16)),
+    (F16, dict(MS=192, KS=NP + 2)),
+    (U16, dict(TL0=96, TL1=96, TL2=96, TR=96, MU=192, AB=96, OU=48)),
 ) for k, n in names.items()}
 PSUM_KEYS = ("pd0", "pd1", "pd2", "pmh", "pmt", "px", "py", "pz")
 SCRATCH.update({k: ("psum", [128, 512], F32) for k in PSUM_KEYS})
-SEMAPHORES = ["cv", "cs", "ct", "cg", "sent",
-              "dtd", "dkc", "dmc", "def", "dpc", "dmt", "dys0", "dys1", "dys2", "dyp", "ttx",
-              "tail1", "tail2", "tail3", "sum0", "sum1", "sum2"]
-
-
-def sum_senders(rnd, dst):
-    if dst == 0:
-        return []
-    s = [dst - 1] + list(range(dst - 1))
-    if rnd > 0 and dst < N - 1:
-        s.append(N - 1)
-    return s
-
-
-def bits(engines):
-    m = 0
-    for e in engines:
-        m |= 1 << e
-    return m
+EXCH = dict(a=(12, I32), b=(12, U16), c=(2, F32), d=(12, F32))
+for _k, (_n, _d) in EXCH.items():
+    SCRATCH["DO" + _k] = ("dram", [N, 128, _n], _d)
+    SCRATCH["DI" + _k] = ("dram", [N, 128, _n], _d)
+SEMAPHORES = (["cv", "cs", "ct", "cg", "sent", "dkc", "dmc", "def", "dpc", "dmt", "dtt", "dea", "dys0", "dys1"]
+              + [p + k for k in EXCH for p in ("xo", "xs", "xr", "xi")])
 
 
 def rank_program(g, core, T, topo):
@@ -127,133 +112,109 @@ def rank_program(g, core, T, topo):
     def fill(wr, ap, c):
         op("v", [], wr, lambda: g.vector.memset(ap, c))
 
+    def scan(rd, wr, out, d0, d1, init, o0, o1):
+        op("v", rd, wr, lambda: g.vector.tensor_tensor_scan(out, d0, d1, init, o0, o1))
+
     def act(rd, wr, out, in_, f, **kw):
         op("s", rd, wr, lambda: g.scalar.activation(out, in_, f, **kw))
 
-    def copy(q, rd, wr, out, in_, **kw):
-        if q == "v":
-            cp(rd, wr, out, in_)
-        else:
-            act(rd, wr, out, in_, ACT.Copy, **kw)
+    def iota(wr, out, pattern, base):
+        op("g", [], wr, lambda: g.iota(out, pattern, base, 0, allow_small_or_imprecise_dtypes=True))
 
-    far = topo.engines(core, next(c for c in cores if topo.chip(c) != topo.chip(core)))
-    mate = next(r for r in range(N) if r != rank and topo.chip(cores[r]) == topo.chip(core))
-    whole = topo.engines(core, cores[mate])
-    near = [e for e in whole if e not in far]
-    half = 0 if rank < mate else 1
+    others = [r for r in range(N) if r != rank]
+    away = [r for r in others if topo.chip(cores[r]) != topo.chip(core)]
+    far = topo.engines(core, cores[away[0]])
+    engine = {r: far[n] for n, r in enumerate(away)}
+    for r in others:
+        if r not in engine:
+            engine[r] = next(e for e in topo.engines(core, cores[r]) if e not in far and e not in engine.values())
+    mine = slice(16 * rank, 16 * rank + 16)
 
-    def engines_to(r):
-        return near if r == mate else far
+    def exchange_out(k, q, rd, src):
+        DO, DI = T["DO" + k], T["DI" + k]
+        dmas(q, "xo" + k, rd, ["DO" + k], [(DO[:], src[:])])
+        dmas(q, "xs" + k, rd, ["DS" + k], [(DI[rank], src[mine, :])])
+        before("g", ["DO" + k], [])
+        g.remote_dma_fused([RemoteDMATransfer(dst_ids=[DstId(rid=topo.addr(cores[r])[0], pnc=topo.addr(cores[r])[1])],
+                                              dma_engine_mask=1 << engine[r], remote_sem=T.sem["xr" + k],
+                                              src=DO[r], dst=DI[rank]) for r in others], local_sem=T.sem["sent"])
+        count["sent"] = count.get("sent", 0) + len(others)
+        count["xr" + k] = len(others)
+        writer["DR" + k] = [("xr" + k, len(others))]
 
-    def arrival(s, n, key):
-        count[s] = n
-        writer[key] = [(s, n)]
+    def exchange_in(k, q, wr, dst):
+        dmas(q, "xi" + k, ["DS" + k, "DR" + k], wr, [(dst[:], T["DI" + k][:])])
 
-    def send(rd, src, dsts, s, engines=None):
-        if not dsts:
-            return
-        before("g", rd, [])
-        if len(dsts) == 1:
-            e = engines or engines_to(dsts[0][0])
-            rid, pid, _ = topo.addr(cores[dsts[0][0]])
-            g.remote_dma(dsts[0][1], src, T.sem[s], T.sem["sent"], pid, rid, bits(e))
-            count["sent"] = count.get("sent", 0) + len(e)
-            return
-        tr = []
-        for x in ([d for d in dsts if d[0] != mate], [d for d in dsts if d[0] == mate]):
-            if x:
-                e = engines_to(x[0][0])
-                tr.append(RemoteDMATransfer(dst_ids=[DstId(rid=topo.addr(cores[r])[0], pnc=topo.addr(cores[r])[1]) for r, _ in x],
-                                            dma_engine_mask=bits(e), remote_sem=T.sem[s], src=src, dsts=[ap for _, ap in x]))
-                count["sent"] = count.get("sent", 0) + len(e)
-        g.remote_dma_fused(tr, local_sem=T.sem["sent"])
+    def groups(dst, src):
+        return [(dst[16 * j:16 * j + 16, :], src) for j in range(N)]
 
     TL = [T.TL0, T.TL1, T.TL2, T.YP]
-    LB = [T.LB0, T.LB1, T.LB2]
     WN = [T.W0, T.W1]
     PD = [T.pd0, T.pd1, T.pd2]
-    for r in range(RO):
-        arrival("tail%d" % (r + 1), len(engines_to((rank - 1) % N)), "TLt%d" % (r + 1))
-        if sum_senders(r, rank):
-            arrival("sum%d" % r, sum(len(engines_to(x)) for x in sum_senders(r, rank)), "LBr%d" % r)
-    arrival("ttx", len(whole), "TTx")
-    mine = slice(MH * half, MH * half + MH)
-
-    dmas("s", "dmc", [], ["MC"], [(T.MC[:], T.meth[:])])
-    dmas("y", "dtd", [], ["TD"], [(T.TD[:], T.todo[:])])
-    dmas("s", "dkc", [], [], [(T.KC[j:128:8, :], T.kid[j, mine]) for j in range(4)])
-    dmas("y", "dkc", [], ["KC"], [(T.KC[j:128:8, :], T.kid[j, mine]) for j in range(4, 8)])
-    dmas("y", "def", [], ["EF"], [(T.EF[:], T.eff[:])])
 
     op("g", [], ["CI0"], lambda: g.iota(T.CI[:, 0:1], [[1, 1]], 0, 1))
-    op("g", [], ["IX"], lambda: g.iota(T.IX[:], [[1, 160]], 0, 0, allow_small_or_imprecise_dtypes=True))
-    op("g", [], ["CX"], lambda: g.iota(T.CX[:], [[16, 48]], WDUMMY - KEYADD, 0, allow_small_or_imprecise_dtypes=True))
+    iota(["IX"], T.IX[:], [[1, 160]], 0)
+    iota(["IM"], T.IM[:], [[0, 8], [1, 16]], 0)
+    dmas("s", "dmc", [], ["MC"], [(T.MC[32 * j:32 * j + 32, :], T.meth[rank, :]) for j in range(4)])
+    exchange_out("a", "y", [], T.todo)
+    dmas("s", "dkc", [], ["KC"], [(T.KC[0:32, :], T.kid[rank, :])])
+    dmas("y", "def", [], ["EF"], groups(T.EF, T.eff[mine, :]))
+    exchange_in("a", "y", ["TD"], T.TD)
+    dmas("y", "dpc", [], ["PC"], groups(T.PC, T.pre[mine, :]))
+
     fill(["MT"], T.MT[:], 0.0)
-    act(["MT"], ["MK"], T.MK[:], T.MT[:, 0:H], ACT.Identity, bias=1.0)
-
-    def clear(w):
-        act(["MK"], ["W%da" % w], WN[w][:, 0:H], T.MK[:], ACT.Copy, scale=0.0)
-        act(["MK"], ["W%db" % w], WN[w][:, H:WREAD], T.MK[:, 0:WREAD - H], ACT.Copy, scale=0.0)
-
-    clear(0)
     ts(["CI0"], ["CI1"], T.CI[:, 1:2], T.CI[:, 0:1], 15, ALU.bitwise_and)
     ts(["CI0"], ["CI2"], T.CI[:, 2:3], T.CI[:, 0:1], 112, ALU.bitwise_and)
     ts(["CI0"], ["CI3"], T.CI[:, 3:4], T.CI[:, 0:1], 15, ALU.bitwise_and, 1, ALU.logical_shift_right)
-    fill(["SM0", "SM1", "SM2", "SM3", "SM4", "SM5"], T.SM[:], 0.0)
-    fill(["ZR"], T.ZR[:], 0.0)
+
+    ts(["MC"], ["M2a"], T.M2[0:32, :], T.MC[0:32, :], 4095 - 63, ALU.bitwise_and)
+    ts(["MC"], ["M2b"], T.M2[32:64, :], T.MC[32:64, :], 63, ALU.bitwise_and)
+    ts(["MC"], ["M2c"], T.M2[64:96, :], T.MC[64:96, :], 12, ALU.logical_shift_right, 4095 - 63, ALU.bitwise_and)
+    ts(["MC"], ["M2d"], T.M2[96:128, :], T.MC[96:128, :], 12, ALU.logical_shift_right, 63, ALU.bitwise_and)
     cp(["CI0", "CI1", "CI2", "CI3"], ["CF"], T.CF[:], T.CI[:])
+    cp(["M2a", "M2b", "M2c", "M2d"], ["MD"], T.MD[:], T.M2[:])
+    dmas("s", "dmt", ["MD"], ["MT"], [(T.MT[16 * j:16 * j + 4, :], T.MD[:]) for j in range(N)])
+
     kc, ic, gcol, hc = T.CF[:, 0:1], T.CF[:, 1:2], T.CF[:, 2:3], T.CF[:, 3:4]
-    names = "b16 od sg hb ta t1 g2 g4 g6 r0 r1 tz w1 w2 wa ba sa e6 x0 y0 hib lob".split()
+    names = "b16 od sg hb ta t1 g2 g4 g6 r0 r1 tz ty g7 w1 w2 wa ba sa e6 x0 y0 hib lob".split()
     C = {k: T.CC[:, j:j + 1] for j, k in enumerate(names)}
 
     def col(k, rd, in0, s1, op0, s2=None, op1=None):
         ts(["CF"] + rd, [k], C[k], in0, s1, op0, s2, op1)
 
-    fill(["ET0"], T.ET[:, 0:1], 0.0)
-    fill(["EH0"], T.EH[:, 0:1], 0.0)
-    col("b16", [], gcol, 16.0, ALU.add)
-    ts(["CF", "IX"], ["ID"], T.ID[:], T.IX[:, 0:128], kc, ALU.is_equal)
-    ts(["CF", "IX"], ["NI"], T.NI[:], T.IX[:, 0:128], kc, ALU.is_equal, -1.0, ALU.mult)
-    ts(["CF", "IX"], ["IF"], T.IF[:], T.IX[:, 0:128], kc, ALU.is_equal)
-
-    ts(["MC"], ["M2a"], T.M2[:, 0:192], T.MC[:], 4095 - 63, ALU.bitwise_and)
-    ts(["MC"], ["M2b"], T.M2[:, 192:384], T.MC[:], 63, ALU.bitwise_and)
-    ts(["MC"], ["M2c"], T.M2[:, 384:576], T.MC[:], 12, ALU.logical_shift_right, 4095 - 63, ALU.bitwise_and)
-    cp(["M2a", "M2b"], ["MDa"], T.MD[:, 0:384], T.M2[:, 0:384])
-    ts(["MC"], ["M2d"], T.M2[:, 576:768], T.MC[:], 12, ALU.logical_shift_right, 63, ALU.bitwise_and)
-    cp(["TD"], ["TLt0", "TLh0"], T.TL0[:, 0:96], T.TD[:])
-    cp(["M2c", "M2d"], ["MDb"], T.MD[:, 384:768], T.M2[:, 384:768])
-    dmas("y", "dmt", ["MDa"], ["MT"], [(T.MT[i:128:16, :], T.MD[:, 192 * i:192 * i + 192]) for i in (0, 1)])
-    dmas("y", "dmt", ["MDb"], ["MTb"], [(T.MT[i:128:16, :], T.MD[:, 192 * i:192 * i + 192]) for i in (2, 3)])
-    writer["MT"] = writer["MTb"]
-    dmas("y", "dpc", [], ["PC"], [(T.PC[:], T.pre[:])])
-
-    def piece(b, j):
-        return b[:, 128 * j:128 * j + 128]
+    def piece(b, j, n=1):
+        return b[:, 32 * j:32 * (j + n)]
 
     def row(i):
-        return T.ST[:, i:MH:16]
+        return piece(T.ST, i)
 
-    ts(["KC"], ["K2a"], T.K2[:, 0:128], T.KC[:], 4095, ALU.bitwise_and)
-    ts(["KC"], ["K2b"], T.K2[:, 128:256], T.KC[:], 12, ALU.logical_shift_right)
+    def wide(b, j):
+        return b[:, 128 * j:128 * j + 128]
+
+    ts(["KC"], ["K2a"], T.K2[0:32, 0:128], T.KC[0:32, :], 4095, ALU.bitwise_and)
+    ts(["KC"], ["K2b"], T.K2[0:32, 128:256], T.KC[0:32, :], 12, ALU.logical_shift_right)
+    ts(["CF", "IX"], ["IF"], T.IF[:], T.IX[:, 0:32], kc, ALU.is_equal)
+    ts(["CF", "IM"], ["L1"], T.L1[:], T.IM[:], ic, ALU.is_equal)
+    ts(["K2a", "K2b"], ["UF"], T.UF[0:32, :], T.K2[0:32, :], -1.0 / 64, ALU.mult, EMPTY / 64.0, ALU.add)
+    mm(["UF", "IF"], ["pd0"], *[[(piece(T.pd0, j), T.UF[0:32, 128 * j:128 * j + 128], T.IF[0:32, :])] for j in range(2)])
+    op("g", ["L1"], ["LOW"], lambda: g.affine_select(T.LOW[:], T.L1[:], [[1, 128]], ALU.is_gt, 0.0, 0, -1))
+    iota(["ZW"], T.ZW[:], [[0, V]], 0)
+    iota(["CX"], T.CX[:], [[16, 48]], WDUMMY - KEYADD)
+
+    def clear(w):
+        iota(["W%d" % w], WN[w][:, 0:WREAD], [[0, WREAD]], 0)
+
+    clear(0)
+    ts(["CF", "IX"], ["ID"], T.ID[:], T.IX[:, 0:128], kc, ALU.is_equal)
+    ts(["CF", "IX"], ["NI"], T.NI[:], T.IX[:, 0:128], kc, ALU.is_equal, -1.0, ALU.mult)
+    col("b16", [], gcol, 16.0, ALU.add)
     ts(["CF", "IX"], ["TG0"], T.TG0[:], T.IX[:, 0:8], hc, ALU.subtract, 1000.0, ALU.mult)
-    ts(["K2a", "K2b"], ["UF"], T.UF[:], T.K2[:], -1.0 / 64, ALU.mult, EMPTY / 64.0, ALU.add)
-    mm(["UF", "IF"], ["pd0"], *[[(piece(T.pd0, j), piece(T.UF, j), T.IF[:])] for j in range(2)])
+    fill(["ST14"], piece(T.ST, 14, 2), 0.0)
+    ts(["pd0"], ["DGh"], T.DG[:, 0:64], T.pd0[:, 0:64], RND, ALU.add, RND, ALU.subtract)
+    ts(["pd0"], ["pd1"], T.pd1[:, 0:64], T.pd0[:, 0:64], 0.0, ALU.is_gt)
+    ts(["pd0"], ["ZS"], T.ZS[:], T.pd0[:, 0:64], 0.0, ALU.is_gt)
     ts(["TG0", "b16"], ["TG"], T.TG[:], T.TG0[:], C["b16"], ALU.add)
-    fill(["ST14"], row(14), 0.0)
-    fill(["ST15"], row(15), 0.0)
-    ts(["TG", "IX"], ["ZM0"], T.ZM0[:], T.IX[:, 0:144], T.TG[:, 0:1], ALU.is_equal)
-    ts(["TG", "IX"], ["ZM1"], T.ZM1[:], T.IX[:, 0:144], T.TG[:, 1:2], ALU.is_equal)
-    fill(["MK"], T.MK[:, 0:H:CH], 0.0)
-    ts(["b16", "IX"], ["ZO"], T.ZO[:], T.IX[:, 0:144], C["b16"], ALU.is_equal)
-    fill(["THa"], T.TH[:, 0:64], -16.0)
-    fill(["THb"], T.TH[:, 64:96], 0.0)
-    for r in range(RO):
-        fill(["LBx%d" % r], LB[r][:, 16:17], 0.0)
-    ts(["pd0"], ["DGh"], T.DG[:, 0:256], T.pd0[:, 0:256], RND, ALU.add, RND, ALU.subtract)
-    ts(["pd0"], ["pd1"], T.pd1[:, 0:256], T.pd0[:, 0:256], 0.0, ALU.is_gt)
-    ts(["pd0"], ["ZS"], T.ZS[:], T.pd0[:, 0:256], 0.0, ALU.is_gt)
-    tt(["pd0", "DGh"], ["DGl"], T.DG[:, 256:512], T.DG[:, 0:256], T.pd0[:, 0:256], ALU.subtract)
+    tt(["pd0", "DGh"], ["DGl"], T.DG[:, 64:128], T.DG[:, 0:64], T.pd0[:, 0:64], ALU.subtract)
     tt(["pd1", "ZS"], ["ST12"], row(12), piece(T.pd1, 0), piece(T.ZS, 1), ALU.add)
     tt(["pd1", "ZS"], ["ST13"], row(13), piece(T.pd1, 0), piece(T.ZS, 1), ALU.max)
     for i, z, d in ((0, 1, 0), (6, 0, 1), (1, 1, 2), (7, 0, 3)):
@@ -269,20 +230,18 @@ def rank_program(g, core, T, topo):
     mm(kk, ["pd2"], *[both(piece(T.pd2, j), d, i) for j, (d, i) in enumerate(((0, 0), (2, 1), (0, 6), (2, 7)))])
     mm(kk, ["px"], *([plus(piece(T.px, j), j) + plus(piece(T.px, j), 13) for j in range(2)]
                      + [both(piece(T.px, 2 + j), 2 * j, j) + plus(piece(T.px, 2 + j), 13) for j in range(2)]))
-    TB = ((T.pz, "pz", "v"), (T.pd0, "pd0", "s"), (T.pd1, "pd1", "v"), (T.pd2, "pd2", "s"))
+    act(["pd2"], ["ST2"], piece(T.ST, 2, 4), piece(T.pd2, 0, 4), ACT.Copy)
+    act(["px"], ["ST8"], piece(T.ST, 8, 4), piece(T.px, 0, 4), ACT.Copy)
+    mm(kk + ["ST2", "ST8", "ST12", "ST14"], ["pmt"], *[[(wide(T.pmt, b), T.ST[:, b:512:4], T.ID[:])] for b in range(4)])
+    act(["pmt"], ["O1"], T.O1[:], T.pmt[:], ACT.Copy)
+    dmas("y", "dtt", ["O1"], ["TT"], groups(T.TT, T.O1[:]))
+    dmas("y", "dea", ["TT"], ["EA"], [(T.EA[:], T.eff[:])])
 
-    def kid_rows():
-        for j in range(4):
-            act(["pd2"], ["ST%d" % (2 + j)], row(2 + j), piece(T.pd2, j), ACT.Copy)
-        for j in range(4):
-            act(["px"], ["ST%d" % (8 + j)], row(8 + j), piece(T.px, j), ACT.Copy)
-
-    def kid_table():
-        for b, (bank, bk, q) in enumerate(TB):
-            mm(["ST%d" % i for i in range(16)] + ["ID"], [bk], *[[(piece(bank, j), piece(T.ST, 4 * b + j), T.ID[:])] for j in range(4)])
-        for b, (bank, bk, q) in enumerate(TB):
-            copy(q, [bk], ["TT%d" % b], T.TT[:, MH * half + 512 * b:MH * half + 512 * b + 512], bank[:])
-        send(["TT%d" % b for b in range(4)], T.TT[:, mine], [(mate, T.TT[:, mine])], "ttx", whole)
+    ts(["TG", "IX"], ["ZM0"], T.ZM0[:], T.IX[:, 0:144], T.TG[:, 0:1], ALU.is_equal)
+    ts(["TG", "IX"], ["ZM1"], T.ZM1[:], T.IX[:, 0:144], T.TG[:, 1:2], ALU.is_equal)
+    fill(["E0"], T.EB[:, 0:1], 0.0)
+    ts(["b16", "IX"], ["ZO"], T.ZO[:], T.IX[:, 0:144], C["b16"], ALU.is_equal)
+    ts(["b16", "IX"], ["ZN"], T.ZN[:], T.IX[:, 0:144], C["b16"], ALU.is_equal, -2.0, ALU.mult)
 
     col("od", [], hc, -2.0, ALU.mult, ic, ALU.add)
     col("hb", [], hc, gcol, ALU.add, 8.0, ALU.add)
@@ -290,224 +249,188 @@ def rank_program(g, core, T, topo):
     col("g2", [], hc, 2.0, ALU.is_ge)
     col("g4", [], hc, 4.0, ALU.is_ge)
     col("g6", [], hc, 6.0, ALU.is_ge)
+    col("g7", [], gcol, 112.0, ALU.is_ge, -128.0, ALU.mult)
     col("wa", [], ic, -2.0, ALU.mult, 25.0, ALU.add)
-    col("ta", ["od", "hb"], C["od"], 1000.0, ALU.mult, C["hb"], ALU.add)
-    col("ba", ["g2", "g4"], C["g2"], C["g4"], ALU.subtract)
-    fill(["VT"], T.VT[:], 0.0)
+    cp(["TD"], ["TLt0", "TLh0"], T.TL0[:], T.TD[:])
 
     def late_constants():
+        col("ta", ["od", "hb"], C["od"], 1000.0, ALU.mult, C["hb"], ALU.add)
+        col("ba", ["g2", "g4"], C["g2"], C["g4"], ALU.subtract)
+        fill(["VT"], T.VT[:], 0.0)
         col("sg", ["od"], C["od"], -2.0, ALU.mult, 1.0, ALU.add)
         col("r0", ["g4", "g2"], C["g4"], -3.0, ALU.mult, C["g2"], ALU.subtract)
         col("r1", ["g6", "b16"], C["g6"], 1000.0, ALU.mult, C["b16"], ALU.add)
-        ts(["CF", "IX"], ["TI0"], T.TI0[:], T.IX[:, 12:14], ic, ALU.subtract, 1000.0, ALU.mult)
+        ts(["ta", "IX"], ["PA"], T.PA[:], T.IX[:, 0:136], C["ta"], ALU.is_equal)
+        ts(["ta", "IX"], ["PB"], T.PB[:], T.IX[:, 0:136], 1000.0, ALU.add, C["ta"], ALU.is_equal)
         col("w2", ["sg", "g4"], C["sg"], C["g4"], ALU.mult, 2.0, ALU.mult)
         col("tz", ["r0", "r1"], C["r0"], hc, ALU.add, C["r1"], ALU.add)
         col("e6", ["ba"], hc, 6.0, ALU.is_equal, C["ba"], ALU.add)
         col("y0", ["g4", "g6"], C["g4"], C["g6"], ALU.subtract, 0.5, ALU.mult)
         col("w1", ["w2", "sg"], C["w2"], -1.5, ALU.mult, C["sg"], ALU.add)
-        ts(["ta", "IX"], ["PA"], T.PA[:], T.IX[:, 0:136], C["ta"], ALU.is_equal)
-        ts(["ta", "IX"], ["PB"], T.PB[:], T.IX[:, 0:136], 1000.0, ALU.add, C["ta"], ALU.is_equal)
-        ts(["TI0", "b16"], ["TI"], T.TI[:], T.TI0[:], C["b16"], ALU.add)
+        col("ty", ["tz", "g7"], C["tz"], 16.0, ALU.add, C["g7"], ALU.add)
         col("x0", ["e6", "t1"], C["e6"], 10000.0, ALU.mult, C["t1"], ALU.add)
         col("sa", ["ba"], ic, 13.0, ALU.is_lt, C["ba"], ALU.subtract)
         col("lob", ["ba", "t1"], C["ba"], -10000.0, ALU.mult, C["t1"], ALU.add)
-        fill(["Z1a"], T.Z1[:, 0:1], 0.0)
-        ts(["tz", "w2", "IX"], ["Z2"], T.Z2[:], T.IX[:, 0:148], C["tz"], ALU.is_equal, C["w2"], ALU.mult)
-        ts(["tz", "w1", "IX"], ["Z1"], T.Z1[:, 1:148], T.IX[:, 0:147], C["tz"], ALU.is_equal, C["w1"], ALU.mult)
         col("hib", ["x0", "y0"], C["x0"], C["y0"], ALU.add)
-        fill(["G0"], T.G2[:, NP:GBO], 0.0)
+
+    def read_selectors(z1, z2, zt, lt, t, k):
+        fill([k + "1a"], z1[:, 0:1], 0.0)
+        ts([t, "w2", "IX"], [k + "2"], z2[:], T.IX[:, 0:148], C[t], ALU.is_equal, C["w2"], ALU.mult)
+        ts([t, "w1", "IX"], [k + "1"], z1[:, 1:148], T.IX[:, 0:147], C[t], ALU.is_equal, C["w1"], ALU.mult)
+        tt([k + "1", k + "1a", k + "2"], [k + "T"], zt[:], z1[:], z2[:], ALU.add)
+        for n, q in enumerate((13, 14, 15)):
+            op("g", [k + "T"], [k + "a%d" % q],
+               lambda: g.affine_select(wide(lt, 2 * n), zt[:, 16 - q:144 - q], [[0, 8], [1, 16]], ALU.is_ge, 0.0, -8, 0))
+            op("g", [k + "T"], [k + "b%d" % q],
+               lambda: g.affine_select(wide(lt, 2 * n + 1), zt[:, 32 - q:160 - q], [[0, 8], [-1, 16]], ALU.is_gt, 0.0, 8, 0))
 
     def selectors(step):
         if step == 0:
-            ts(["TG", "wa", "IX"], ["ZA"], T.ZA[:], T.IX[:, 0:144], T.TG[:, 6:7], ALU.is_equal, C["wa"], ALU.mult)
-            ts(["TI", "IX"], ["ZB"], T.ZB[:], T.IX[:, 1:145], T.TI[:, 1:2], ALU.is_equal)
+            read_selectors(T.Z1, T.Z2, T.ZT, T.LT, "tz", "Z")
         elif step == 1:
+            ts(["CF", "IX"], ["TI0"], T.TI0[:], T.IX[:, 12:14], ic, ALU.subtract, 1000.0, ALU.mult)
+            fill(["G0"], T.G2[:, NP:GBO], 0.0)
+            ts(["TG", "wa", "IX"], ["ZA"], T.ZA[:], T.IX[:, 0:144], T.TG[:, 6:7], ALU.is_equal, C["wa"], ALU.mult)
+            ts(["TI0", "b16"], ["TI"], T.TI[:], T.TI0[:], C["b16"], ALU.add)
+            ts(["CF", "CX"], ["CD"], T.CD[:], T.CX[:], ic, ALU.add)
+            ts(["TI", "IX"], ["ZB"], T.ZB[:], T.IX[:, 1:145], T.TI[:, 1:2], ALU.is_equal)
             ts(["TI", "IX"], ["ZE"], T.ZE[:], T.IX[:, 0:144], T.TI[:, 0:1], ALU.is_equal, -8192.0, ALU.mult)
             tt(["ZA", "ZB"], ["ZC"], T.ZC[:], T.ZA[:], T.ZB[:], ALU.add)
         else:
-            tt(["Z1", "Z1a", "Z2"], ["ZT"], T.ZT[:], T.Z1[:], T.Z2[:], ALU.add)
-            ts(["CF", "CX"], ["CD"], T.CD[:], T.CX[:], ic, ALU.add)
-            for n, q in enumerate((13, 14, 15)):
-                op("g", ["ZT"], ["LTa%d" % q],
-                   lambda: g.affine_select(piece(T.LT, 2 * n), T.ZT[:, 16 - q:144 - q], [[0, 8], [1, 16]], ALU.is_ge, 0.0, -8, 0))
-                op("g", ["ZT"], ["LTb%d" % q],
-                   lambda: g.affine_select(piece(T.LT, 2 * n + 1), T.ZT[:, 32 - q:160 - q], [[0, 8], [-1, 16]], ALU.is_gt, 0.0, 8, 0))
+            read_selectors(T.Y1, T.Y2, T.YT, T.LY, "ty", "Y")
+            clear(1)
 
     def sel(z, q):
         return z[:, 16 - q:144 - q]
 
+    LB = dict(a="py", b="px", t="pmh")
+
     def part_of(part):
         lo = 32 * "tab".index(part)
-        return lo, slice(16 * lo, 16 * lo + A), "SRt" if part == "t" else "SRh"
+        return lo, slice(16 * lo, 16 * lo + A)
 
-    def gather_methods(q, tl, key, part):
-        lo, c, _ = part_of(part)
-        copy(q, [key, "MT"], ["MG" + part], T.MG[:, c], T.MT[:, :].indirect(tl[:, lo:lo + 32]))
+    def gather_methods(tl, key, part):
+        lo, c = part_of(part)
+        cp([key, "MT"], ["MG" + part], T.MG[:, c], T.MT[:, :].indirect(tl[:, lo:lo + 32]))
 
-    def method_list(part, j, bk):
-        lo = part_of(part)[0]
-        z, zk = ((T.ZM0, "ZM0"), (T.ZM1, "ZM1"))[j]
-        mm(["MG" + part, zk], [bk], [(T[bk][:, 0:32], sel(z, q), T.MG[:, 16 * lo + q:16 * lo + A:16]) for q in range(16)])
+    def method_lists(part):
+        lo, bk = part_of(part)[0], LB[part]
+        mm(["MG" + part, "ZM0", "ZM1"], [bk],
+           *[[(piece(T[bk], j), sel(z, q), T.MG[:, 16 * lo + q:16 * lo + A:16]) for q in range(16)]
+             for j, z in enumerate((T.ZM0, T.ZM1))])
 
-    def method_offsets(part, j, bk):
-        lo = part_of(part)[0]
-        cp([bk], ["MU%d%s" % (j, part)], T.MU[:, 96 * j + lo:96 * j + lo + 32], T[bk][:, 0:32])
+    def method_offsets(part):
+        lo, bk = part_of(part)[0], LB[part]
+        for j in (1, 0):
+            cp([bk], ["MU%d%s" % (j, part)], T.MU[:, 96 * j + lo:96 * j + lo + 32], piece(T[bk], j))
 
-    def scan(part):
-        e, a, n = (T.ET, 0, A) if part == "t" else (T.EH, A, H)
-        op("v", ["E" + part, "ET0", "EH0", "MK"], ["SR" + part],
-           lambda: g.vector.tensor_tensor_scan(T.SR[:, a:a + n], e[:, 0:n], T.MK[:, 0:n], 0.0, ALU.add, ALU.mult))
-
-    def diff0(part):
-        lo, c, sr = part_of(part)
-        tt(["MU0" + part, "PC", sr], ["D0" + part], T.D0[:, c], T.PC[:, :].indirect(T.MU[:, lo:lo + 32]), T.SR[:, c], ALU.subtract)
+    def vote0(part):
+        lo, c = part_of(part)
+        tt(["MU0" + part, "PC", "SB"], ["B0" + part], T.B0[:, c], T.PC[:, :].indirect(T.MU[:, lo:lo + 32]), T.SB[:, c], ALU.is_le)
 
     def cond1(part):
-        lo, c, sr = part_of(part)
+        lo, c = part_of(part)
         act(["MU1" + part, "PC"], ["P1" + part], T.P1[:, c], T.PC[:, :].indirect(T.MU[:, 96 + lo:96 + lo + 32]), ACT.Copy)
 
     def diff1(part):
-        lo, c, sr = part_of(part)
+        lo, c = part_of(part)
         k = lo // 32
-        mm([sr, "P1" + part, "NI", "ID"], ["pd%d" % k], [(PD[k][:], T.NI[:], T.SR[:, c]), (PD[k][:], T.ID[:], T.P1[:, c])])
+        mm(["SB", "P1" + part, "NI", "ID"], ["pd%d" % k], [(PD[k][:], T.NI[:], T.SB[:, c]), (PD[k][:], T.ID[:], T.P1[:, c])])
+
+    def vote1(part):
+        lo, c = part_of(part)
+        act(["pd%d" % (lo // 32), "half"], ["B1" + part], T.B1[:, c], PD[lo // 32][:], ACT.Sign, bias=T.CC[:, 31:32], scale=-1.0)
+
+    def votes(parts, j):
+        lo, n = part_of(parts[0])[0], 32 * len(parts)
+        b, z, zk = ((T.B0, T.ZN, "ZN"), (T.B1, T.ZO, "ZO"))[j]
+        mm(["B%d%s" % (j, p) for p in parts] + [zk], ["px"],
+           [(T.px[:, lo:lo + n], sel(z, q), b[:, 16 * lo + q:16 * (lo + n):16]) for q in range(16)], first=j == 0, last=j == 1)
 
     def row_list(rnd, part):
-        lo, n, bank, bk = (0, 64, T.pz, "pz") if part == "h" else (64, 32, T.pmt, "pmt")
+        lo, n, bank, bk, zt, lt, k = (0, 64, T.pz, "pz", T.ZT, T.LT, "Z") if part == "h" else (64, 32, T.pmt, "pmt", T.YT, T.LY, "Y")
         win, items = WN[rnd % 2], []
         for q in range(16):
-            items.append((bank[:, 0:n], sel(T.ZT, q) if q < 13 else piece(T.LT, 2 * (q - 13)), win[:, 16 * (lo + 1) + q:16 * (lo + n + 1):16]))
+            items.append((bank[:, 0:n], sel(zt, q) if q < 13 else wide(lt, 2 * (q - 13)), win[:, 16 * (lo + 1) + q:16 * (lo + n + 1):16]))
         for q in (13, 14, 15):
-            items.append((bank[:, 0:n], piece(T.LT, 2 * (q - 13) + 1), win[:, 16 * lo + q:16 * (lo + n):16]))
-        mm(["W%da" % (rnd % 2), "W%db" % (rnd % 2), "ZT"] + ["LT%s%d" % (x, q) for x in "ab" for q in (13, 14, 15)], [bk], items)
+            items.append((bank[:, 0:n], wide(lt, 2 * (q - 13) + 1), win[:, 16 * lo + q:16 * (lo + n):16]))
+        mm(["W%d" % (rnd % 2), k + "T"] + ["%s%s%d" % (k, x, q) for x in "ab" for q in (13, 14, 15)], [bk], items)
 
     def row_types(rnd, part):
-        lo, n, bank, bk = (0, 64, T.pz, "pz") if part == "h" else (64, 32, T.pmt, "pmt")
-        key = "TL%s%d" % (part, rnd + 1)
-        ts([bk], [key], TL[rnd + 1][:, 32 + lo:32 + lo + n], bank[:, 0:n], -64.0, ALU.mult, float(EMPTY), ALU.add)
-        if part == "o":
-            send([key], TL[rnd + 1][:, 96:128], [((rank + 1) % N, TL[rnd + 1][:, 0:32])], "tail%d" % (rnd + 1))
+        lo, n, bank, bk = (32, 64, T.pz, "pz") if part == "h" else (0, 32, T.pmt, "pmt")
+        ts([bk], ["TL%s%d" % (part, rnd + 1)], TL[rnd + 1][:, lo:lo + n], bank[:, 0:n], -64.0, ALU.mult, float(EMPTY), ALU.add)
 
-    lastrank = rank == N - 1
     GA, GB = T.G2[:, 0:NP], T.G2[:, GBO:GBO + NP]
     for rnd in range(RO):
-        tl, lb, win = TL[rnd], LB[rnd], WN[rnd % 2]
-        kt, kh, ko = "TLt%d" % rnd, "TLh%d" % rnd, "TLo%d" % rnd
-        st, sh = "SM%d" % (2 * rnd), "SM%d" % (2 * rnd + 1)
-        sumt, sumh = T.SM[:, 2 * rnd:2 * rnd + 1], T.SM[:, 2 * rnd + 1:2 * rnd + 2]
-        dsts = []
-        for d in (range(N) if lastrank else range(N - 1, -1, -1)):
-            s = sum_senders(rnd, d)
-            if rank in s:
-                c = 16 - 2 * len(s) + 2 * s.index(rank)
-                dsts.append((d, lb[:, c:c + 2]))
+        tl, win = TL[rnd], WN[rnd % 2]
+        kt, kh = "TLt%d" % rnd, "TLh%d" % rnd
+        last = rnd == RO - 1
 
-        def effects(q, key, wr, out, lo, n, sk=None, acc=None):
-            kw = {"accum_out": acc} if sk else {}
-            copy(q, [key, "EF"], [wr] + ([sk] if sk else []), out, T.EF[:, :].indirect(tl[:, lo:lo + n]), **kw)
-
-        gather_methods("v", tl, kh, "a")
+        gather_methods(tl, kh, "a")
         if rnd > 0:
-            row_types(rnd - 1, "o")
-        effects("s", kh, "Eh", T.EH[:, 1:H + 1], 32, 64, None if lastrank else sh, sumh)
+            row_types(rnd - 1, "t")
+        if last:
+            exchange_out("b", "y", [kt, kh], tl)
+            exchange_in("b", "y", ["TR"], T.TR)
+        act([kh, "EF"], ["Eh", "SMh"], T.EB[:, A + 1:V + 1], T.EF[:, :].indirect(tl[:, 32:96]), ACT.Copy, accum_out=T.SM[:, 0:1])
+        act([kt, "EF"], ["Et", "SMt"], T.EB[:, 1:A + 1], T.EF[:, :].indirect(tl[:, 0:32]), ACT.Copy, accum_out=T.SM[:, 1:2])
+        method_lists("a")
+        gather_methods(tl, kh, "b")
+        method_lists("b")
+        method_offsets("a")
+        gather_methods(tl, kt, "t")
+        for bank, bk in ((T.pz, "pz"), (T.pmt, "pmt"))[:2 if last else 1]:
+            mm(["SMh", "SMt", "LOW"], [bk], [(bank[:, 128:129], T.LOW[:], T.SM[:, j:j + 1]) for j in range(2)])
+        method_lists("t")
+        method_offsets("b")
         if rnd == 0:
-            effects("s", kt, "Et", T.ET[:, 1:A + 1], 0, 32, None if lastrank else st, sumt)
-        elif rank != N - 2:
-            effects("s", ko, "EJ", T.EJ[:], 96, 32, st, sumt)
-        send([st, sh], T.SM[:, 2 * rnd:2 * rnd + 2], dsts, "sum%d" % rnd)
-        method_list("a", 0, "pmh")
-        method_list("a", 1, "py")
-        gather_methods("v", tl, kh, "b")
-        if rnd == 0:
-            kid_rows()
-            gather_methods("s", tl, kt, "t")
-        method_list("b", 0, "px")
-        method_list("b", 1, "pmt")
-        method_offsets("a", 0, "pmh")
-        method_offsets("a", 1, "py")
-        scan("h")
-        if rnd == 0:
-            method_offsets("b", 0, "px")
-            method_offsets("b", 1, "pmt")
-            kid_table()
-            cond1("a")
-            diff0("a")
-        else:
-            cond1("a")
-            diff0("a")
-            method_offsets("b", 0, "px")
-            method_offsets("b", 1, "pmt")
-            gather_methods("s", tl, kt, "t")
+            fill(["half"], T.CC[:, 31:32], 0.5)
+            fill(["XB0"], T.XB[:], 0.0)
+            fill(["EY0"], T.EY[:, 0:1], 0.0)
+        scan(["Eh", "Et", "E0", "ZW", "pz"], ["SB"], T.SB[:], T.EB[:, 0:V], T.ZW[:], T.pz[:, 128:129], ALU.add, ALU.add)
+        method_offsets("t")
+        cond1("a")
+        if last:
+            act(["pmt", "XB0"], ["XB"], T.XB[:, 0:1], T.pmt[:, 128:129], ACT.Copy)
+            exchange_out("c", "y", ["XB"], T.XB)
+            exchange_in("c", "y", ["XR"], T.XR)
+        for p in "abt":
+            vote0(p)
         diff1("a")
-        method_list("t", 1, "py")
-        method_list("t", 0, "pmh")
         cond1("b")
-        diff0("b")
-        if rnd > 0:
-            effects("v", kt, "Et", T.ET[:, 1:A + 1], 0, 32)
-        method_offsets("t", 1, "py")
-        cond1("t")
         diff1("b")
-        scan("t")
-        method_offsets("t", 0, "pmh")
-        tt(["SRh", "Eh"], ["CTh"], lb[:, 21:28], T.SR[:, A + CH - 1:V - 1:CH], T.EH[:, CH:H:CH], ALU.add)
-        tt(["SRt", "Et"], ["CTt"], lb[:, 17:21], T.SR[:, CH - 1:A:CH], T.ET[:, CH:A + 1:CH], ALU.add)
-        if lastrank and rnd > 0:
-            cp([st], ["LBx%d" % rnd], lb[:, 16:17], sumt)
+        cond1("t")
         diff1("t")
-        diff0("t")
-
-        ns = len(sum_senders(rnd, rank))
-        c0 = 16 - 2 * ns + (1 if (rnd > 0 and ns) else 0)
-        op("v", ["LBr%d" % rnd, "LBx%d" % rnd, "CTt", "CTh", "ZR"], ["BS"],
-           lambda: g.vector.tensor_tensor_scan(T.BS[:, c0:28], lb[:, c0:28], T.ZR[:, c0:28], 0.5, ALU.add, ALU.add))
+        for p in "abt":
+            vote1(p)
+        votes("ab", 0)
+        votes("ab", 1)
+        votes("t", 0)
+        votes("t", 1)
         ts(["MU1t", "MU1a", "MU1b"], ["MF"], T.MF[:], T.MU[:, 96:192], -2048.0, ALU.add)
-
-        def chunk(k):
-            return slice(CH * k, CH * k + CH), slice(CH * (k % 4), CH * (k % 4) + CH), T.BS[:, 16 + k:17 + k]
-
-        for k in (4, 5, 6, 7, 0, 1, 2, 3):
-            c, p, b = chunk(k)
-            act(["BS", "pd%d" % (k // 4)], ["B1%d" % k], T.B1[:, c], PD[k // 4][:, p], ACT.Sign, bias=b, scale=-1.0)
-        for k in range(NCH):
-            c, p, b = chunk(k)
-            ts(["BS", "D0t", "D0a", "D0b"], ["B0%d" % k], T.B0[:, c], T.D0[:, c], b, ALU.is_le, -2.0, ALU.mult)
-        for k in range(8, NCH):
-            c, p, b = chunk(k)
-            ts(["BS", "pd2"], ["B1%d" % k], T.B1[:, c], PD[2][:, p], b, ALU.is_le, 2.0, ALU.mult)
-        mm(["B0%d" % k for k in range(NCH)] + ["ZO"], ["px"], [(T.px[:, 0:96], sel(T.ZO, q), T.B0[:, q:V:16]) for q in range(16)], last=False)
-        mm(["B1%d" % k for k in range(NCH)], ["px"], [(T.px[:, 0:96], sel(T.ZO, q), T.B1[:, q:V:16]) for q in range(16)], first=False)
         ts(["MU0t", "MU0a", "MU0b"], ["pmh"], T.pmh[:, 1:192:2], T.MU[:, 0:96], -2048.0, ALU.add)
-        if rnd == RO - 1:
-            ts(["BS"], ["BX"], T.BX[:, 0:NCH], T.BS[:, 16:28], -0.5, ALU.add)
         if rnd == 0:
             late_constants()
         tt(["MF", "pmh"], ["DM"], T.pmh[:, 0:192:2], T.MF[:], T.pmh[:, 1:192:2], ALU.subtract)
+        if last:
+            act(["TR", "EA"], ["EYa"], T.EY[:, 1:NP + 1], T.EA[:, :].indirect(T.TR[:, 0:48]), ACT.Copy)
 
-        tt(["px", "THa", "THb"], ["VT"], T.VT[:, 1:192:2], T.px[:, 0:96], T.TH[:], ALU.is_gt)
-        if rnd == 0:
-            selectors(0)
-        op("v", ["VT", "DM", "pmh"], ["MS"],
-           lambda: g.vector.tensor_tensor_scan(T.MS[:], T.VT[:], T.pmh[:, 0:192], 0.0, ALU.mult, ALU.add))
+        ts(["px"], ["VT"], T.VT[:, 1:192:2], T.px[:, 0:96], -16.0, ALU.is_gt)
+        scan(["VT", "DM", "pmh"], ["MS"], T.MS[:], T.VT[:], T.pmh[:, 0:192], 0.0, ALU.mult, ALU.add)
         mm(["MS", "PA", "PB"], ["py"], *[[(T.py[:, 48 * j:48 * j + 48], z[:, 8:136], T.MS[:, 1:192:4]),
                                           (T.py[:, 48 * j:48 * j + 48], z[:, 0:128], T.MS[:, 3:192:4])] for j, z in enumerate((T.PA, T.PB))])
         if rnd == 0:
-            selectors(1)
+            selectors(0)
         ts(["py"], ["AB"], T.AB[:], T.py[:, 0:96], 2048.0, ALU.add)
-        tk = ["AB", "TTx"] + ["TT%d" % b for b in range(4)]
-        act(tk + ["sa", "ba"], ["GA"], GA, T.TT[:, :].indirect(T.AB[:, 0:48]), ACT.Identity, scale=C["sa"], bias=C["ba"])
-        ts(tk + ["hib", "lob"], ["GB"], GB, T.TT[:, :].indirect(T.AB[:, 48:96]), C["hib"], ALU.min, C["lob"], ALU.max)
-        if rnd == RO - 1:
-            for k in range(3):
-                c = slice(512 * k, 512 * k + 512)
-                mm(["SRt", "SRh", "ID"], ["pd%d" % k], [(PD[k][:], T.ID[:], T.SR[:, c])])
-                for j in range(4 * k, 4 * k + 4):
-                    cc, p, _ = chunk(j)
-                    act(["BX", "pd%d" % k], ["YS%d" % j], T.YS[:, cc], PD[k][:, p], ACT.Identity, bias=T.BX[:, j:j + 1])
-                dmas("y", "dys%d" % k, ["YS%d" % j for j in range(4 * k, 4 * k + 4)], [], [(T.ys[:, c], T.YS[:, c])])
+        if rnd == 0:
+            selectors(1)
+        act(["AB", "TT", "sa", "ba"], ["GA"], GA, T.TT[:, :].indirect(T.AB[:, 0:48]), ACT.Identity, scale=C["sa"], bias=C["ba"])
+        ts(["AB", "TT", "hib", "lob"], ["GB"], GB, T.TT[:, :].indirect(T.AB[:, 48:96]), C["hib"], ALU.min, C["lob"], ALU.max)
+        if last:
+            act(["TR", "EA"], ["EYb"], T.EY[:, NP + 1:V + 1], T.EA[:, :].indirect(T.TR[:, 48:96]), ACT.Copy)
 
         mm(["GA", "GB", "G0", "ZE"], ["px"], [(T.px[:, 0:97], sel(T.ZE, q), T.G2[:, q:GBO + NP:16]) for q in range(16)])
-        op("v", ["GA", "GB", "G0"], ["KS"],
-           lambda: g.vector.tensor_tensor_scan(T.KS[:, 0:NP + 1], T.G2[:, 0:NP + 1], T.G2[:, GBO - 1:GBO + NP], -float(KEY0), ALU.add, ALU.add))
+        scan(["GA", "GB", "G0"], ["KS"], T.KS[:, 0:NP + 1], T.G2[:, 0:NP + 1], T.G2[:, GBO - 1:GBO + NP], -float(KEY0), ALU.add, ALU.add)
         mm(["KS", "ZA", "ZB", "ZC"], ["py"],
            [(T.py[:, 0:48], sel(T.ZA if q == 0 else T.ZB if q == 16 else T.ZC, q), T.KS[:, q:q + NP - 15:16]) for q in range(17)])
         if rnd == 0:
@@ -516,18 +439,21 @@ def rank_program(g, core, T, topo):
         tt(["px", "CE0"], ["CE"], T.CE[:], T.px[:, 49:97], T.CE0[:], ALU.add)
         tt(["py", "CE"], ["OF"], T.OF[:], T.py[:, 0:48], T.CE[:], ALU.max)
         ts(["OF"], ["OU"], T.OU[:], T.OF[:], float(KEYADD), ALU.add)
-        tt(["OU", "GA", "GB"], ["W%da" % (rnd % 2), "W%db" % (rnd % 2)], win[:, :].indirect(T.OU[:]), GA, GB, ALU.mult)
+        tt(["OU", "GA", "GB"], ["W%d" % (rnd % 2)], win[:, :].indirect(T.OU[:]), GA, GB, ALU.mult)
 
-        if rnd + 1 < RO:
-            clear((rnd + 1) % 2)
-            row_list(rnd, "h")
-            row_list(rnd, "o")
-            row_types(rnd, "h")
-        else:
-            row_list(rnd, "o")
-            row_list(rnd, "h")
-            row_types(rnd, "o")
+        row_list(rnd, "h")
+        row_list(rnd, "t")
+        if rnd == 0:
+            clear(0)
+        if not last:
             row_types(rnd, "h")
 
-    dmas("y", "dyp", ["TLh%d" % RO, "TLt%d" % RO], [], [(T.yp[:], T.YP[:, 0:96])])
+    scan(["EYa", "EY0", "ZW", "XR"], ["YSa"], T.YS[:, 0:NP], T.EY[:, 0:NP], T.ZW[:, 0:NP], T.XR[:, 0:1], ALU.add, ALU.add)
+    dmas("s", "dys0", ["YSa"], [], [(T.ys[:, 0:NP], T.YS[:, 0:NP])])
+    row_types(RO - 1, "h")
+    row_types(RO - 1, "t")
+    exchange_out("d", "y", ["TLh%d" % RO, "TLt%d" % RO], T.YP)
+    scan(["EYa", "EYb", "ZW", "YSa"], ["YSb"], T.YS[:, NP:V], T.EY[:, NP:V], T.ZW[:, 0:NP], T.YS[:, NP - 1:NP], ALU.add, ALU.add)
+    dmas("s", "dys1", ["YSb"], [], [(T.ys[:, NP:V], T.YS[:, NP:V])])
+    exchange_in("d", "y", [], T.yp)
     wait("y", list(count.items()))

@@ -7,7 +7,6 @@ N, V, A, W, M, RO = 8, 1536, 512, 3072, 4096, 3
 H = V - A
 EMPTY = W - 1
 NP = V // 2
-GBO = NP + 16
 WREAD = V + 16
 WDUMMY = 2 * V + 16
 WCOLS = WDUMMY + NP
@@ -15,17 +14,19 @@ KEY0 = 1024
 KEYADD = KEY0 + 13
 RND = 12582912.0
 F32, BF, F16, I32, U16 = "float32", "bfloat16", "float16", "int32", "uint16"
+STAGES = ("ta", "b")
+ORDER = ("rt gt Et rh Eh lt ga gb ot ct la Ot Z1 Oa x B oa ca S lb Ob ob cb va dt wt vt da wa vb D L db 0ta F 1ta mta Mta Z0 0b wb 1b mb pta qta Ata Mb Gta pb qb kta Ab fta Gb Kta ya nta jta Z2 sta kb yb uta fb jb Uta sb Wta nb ub Ub Wb Y Rt Rh C")
 
 SCRATCH = {k: ("sbuf", [128, n], d) for d, names in (
     (I32, dict(TD=96, KC=128, K2=256, MC=96, M2=96, CI=4)),
     (BF, dict(MD=96, DG=128, ST=512, ZS=64, O1=512, EF=W, EA=W, PC=M, MT=W, TT=M, IX=160, IM=128,
               ZO=144, ZN=144, ZM0=144, ZM1=144, Z1=148, Z2=148, ZT=148, Y1=148, Y2=148, YT=148, LT=768, LY=768,
               ZA=144, ZB=144, ZC=144, ZE=144, PA=136, PB=136,
-              ID=128, NI=128, ZW=V, EB=V + 2, EY=V + 2, MG=V, P1=V, B0=V, B1=V, SB=V, G2=GBO + NP,
+              ID=128, NI=128, ZW=V, EB=V + 2, EY=V + 2, MG=V, P1=V, B0=V, B1=V, SB=V, G2=V + 32,
               W0=WCOLS, W1=WCOLS)),
     (F32, dict(CF=4, CX=48, CD=48, CC=32, TG=8, TG0=8, TI=2, TI0=2, YP=96, YS=V, MF=96, VT=192,
-               CE=48, CE0=48, OF=48, SM=2, UF=256, IF=32, L1=128, LOW=128, XB=16, XR=16)),
-    (F16, dict(MS=192, KS=NP + 2)),
+               CE=48, CE0=48, OF=48, SM=2, UF=256, IF=32, L1=128, LOW=128, XB=16, XR=16, KE=2)),
+    (F16, dict(MS=192, KS=NP + 4)),
     (U16, dict(TL0=96, TL1=96, TL2=96, TR=96, MU=192, AB=96, OU=48)),
 ) for k, n in names.items()}
 PSUM_KEYS = ("pd0", "pd1", "pd2", "pmh", "pmt", "px", "py", "pz")
@@ -155,12 +156,11 @@ def rank_program(g, core, T, topo):
     op("g", [], ["CI0"], lambda: g.iota(T.CI[:, 0:1], [[1, 1]], 0, 1))
     iota(["IX"], T.IX[:], [[1, 160]], 0)
     iota(["IM"], T.IM[:], [[0, 8], [1, 16]], 0)
-    dmas("s", "dmc", [], ["MC"], [(T.MC[32 * j:32 * j + 32, :], T.meth[rank, :]) for j in range(4)])
     exchange_out("a", "y", [], T.todo)
+    dmas("s", "dmc", [], [], [(T.MC[32 * j:32 * j + 32, :], T.meth[rank, :]) for j in (0, 1)])
+    dmas("y", "dmc", [], ["MC"], [(T.MC[32 * j:32 * j + 32, :], T.meth[rank, :]) for j in (2, 3)])
     dmas("s", "dkc", [], ["KC"], [(T.KC[0:32, :], T.kid[rank, :])])
     dmas("y", "def", [], ["EF"], groups(T.EF, T.eff[mine, :]))
-    exchange_in("a", "y", ["TD"], T.TD)
-    dmas("y", "dpc", [], ["PC"], groups(T.PC, T.pre[mine, :]))
 
     fill(["MT"], T.MT[:], 0.0)
     ts(["CI0"], ["CI1"], T.CI[:, 1:2], T.CI[:, 0:1], 15, ALU.bitwise_and)
@@ -174,9 +174,11 @@ def rank_program(g, core, T, topo):
     cp(["CI0", "CI1", "CI2", "CI3"], ["CF"], T.CF[:], T.CI[:])
     cp(["M2a", "M2b", "M2c", "M2d"], ["MD"], T.MD[:], T.M2[:])
     dmas("s", "dmt", ["MD"], ["MT"], [(T.MT[16 * j:16 * j + 4, :], T.MD[:]) for j in range(N)])
+    exchange_in("a", "y", ["TD"], T.TD)
+    dmas("y", "dpc", [], ["PC"], groups(T.PC, T.pre[mine, :]))
 
     kc, ic, gcol, hc = T.CF[:, 0:1], T.CF[:, 1:2], T.CF[:, 2:3], T.CF[:, 3:4]
-    names = "b16 od sg hb ta t1 g2 g4 g6 r0 r1 tz ty g7 w1 w2 wa ba sa e6 x0 y0 hib lob".split()
+    names = "b16 od sg hb ta t1 g2 g4 g6 r0 r1 tz ty g7 w1 w2 wa ba sa e6 x0 y0 hib lob half".split()
     C = {k: T.CC[:, j:j + 1] for j, k in enumerate(names)}
 
     def col(k, rd, in0, s1, op0, s2=None, op1=None):
@@ -263,20 +265,20 @@ def rank_program(g, core, T, topo):
         ts(["ta", "IX"], ["PA"], T.PA[:], T.IX[:, 0:136], C["ta"], ALU.is_equal)
         ts(["ta", "IX"], ["PB"], T.PB[:], T.IX[:, 0:136], 1000.0, ALU.add, C["ta"], ALU.is_equal)
         col("w2", ["sg", "g4"], C["sg"], C["g4"], ALU.mult, 2.0, ALU.mult)
-        col("tz", ["r0", "r1"], C["r0"], hc, ALU.add, C["r1"], ALU.add)
         col("e6", ["ba"], hc, 6.0, ALU.is_equal, C["ba"], ALU.add)
         col("y0", ["g4", "g6"], C["g4"], C["g6"], ALU.subtract, 0.5, ALU.mult)
-        col("w1", ["w2", "sg"], C["w2"], -1.5, ALU.mult, C["sg"], ALU.add)
-        col("ty", ["tz", "g7"], C["tz"], 16.0, ALU.add, C["g7"], ALU.add)
-        col("x0", ["e6", "t1"], C["e6"], 10000.0, ALU.mult, C["t1"], ALU.add)
+        col("tz", ["r0", "r1"], C["r0"], hc, ALU.add, C["r1"], ALU.add)
         col("sa", ["ba"], ic, 13.0, ALU.is_lt, C["ba"], ALU.subtract)
         col("lob", ["ba", "t1"], C["ba"], -10000.0, ALU.mult, C["t1"], ALU.add)
+        col("x0", ["e6", "t1"], C["e6"], 10000.0, ALU.mult, C["t1"], ALU.add)
+        col("w1", ["w2", "sg"], C["w2"], -1.5, ALU.mult, C["sg"], ALU.add)
+        col("ty", ["tz", "g7"], C["tz"], 16.0, ALU.add, C["g7"], ALU.add)
         col("hib", ["x0", "y0"], C["x0"], C["y0"], ALU.add)
 
     def read_selectors(z1, z2, zt, lt, t, k):
         fill([k + "1a"], z1[:, 0:1], 0.0)
-        ts([t, "w2", "IX"], [k + "2"], z2[:], T.IX[:, 0:148], C[t], ALU.is_equal, C["w2"], ALU.mult)
         ts([t, "w1", "IX"], [k + "1"], z1[:, 1:148], T.IX[:, 0:147], C[t], ALU.is_equal, C["w1"], ALU.mult)
+        ts([t, "w2", "IX"], [k + "2"], z2[:], T.IX[:, 0:148], C[t], ALU.is_equal, C["w2"], ALU.mult)
         tt([k + "1", k + "1a", k + "2"], [k + "T"], zt[:], z1[:], z2[:], ALU.add)
         for n, q in enumerate((13, 14, 15)):
             op("g", [k + "T"], [k + "a%d" % q],
@@ -285,14 +287,18 @@ def rank_program(g, core, T, topo):
                lambda: g.affine_select(wide(lt, 2 * n + 1), zt[:, 32 - q:160 - q], [[0, 8], [-1, 16]], ALU.is_gt, 0.0, 8, 0))
 
     def selectors(step):
-        if step == 0:
+        if step == "0":
             read_selectors(T.Z1, T.Z2, T.ZT, T.LT, "tz", "Z")
-        elif step == 1:
+        elif step == "1":
             ts(["CF", "IX"], ["TI0"], T.TI0[:], T.IX[:, 12:14], ic, ALU.subtract, 1000.0, ALU.mult)
-            fill(["G0"], T.G2[:, NP:GBO], 0.0)
+            for s in STAGES:
+                fill(["G0" + s], T.G2[:, stage(s)[3] - 16:stage(s)[3]], 0.0)
             ts(["TG", "wa", "IX"], ["ZA"], T.ZA[:], T.IX[:, 0:144], T.TG[:, 6:7], ALU.is_equal, C["wa"], ALU.mult)
-            ts(["TI0", "b16"], ["TI"], T.TI[:], T.TI0[:], C["b16"], ALU.add)
             ts(["CF", "CX"], ["CD"], T.CD[:], T.CX[:], ic, ALU.add)
+            ts(["TI0", "b16"], ["TI"], T.TI[:], T.TI0[:], C["b16"], ALU.add)
+            fill(["half"], C["half"], 0.5)
+            fill(["XB0"], T.XB[:], 0.0)
+            fill(["EY0"], T.EY[:, 0:1], 0.0)
             ts(["TI", "IX"], ["ZB"], T.ZB[:], T.IX[:, 1:145], T.TI[:, 1:2], ALU.is_equal)
             ts(["TI", "IX"], ["ZE"], T.ZE[:], T.IX[:, 0:144], T.TI[:, 0:1], ALU.is_equal, -8192.0, ALU.mult)
             tt(["ZA", "ZB"], ["ZC"], T.ZC[:], T.ZA[:], T.ZB[:], ALU.add)
@@ -303,157 +309,147 @@ def rank_program(g, core, T, topo):
     def sel(z, q):
         return z[:, 16 - q:144 - q]
 
-    LB = dict(a="py", b="px", t="pmh")
+    LB = dict(t="py", a="pmt", b="px")
+    BK = dict(zip(STAGES, (("pz", "py", "pd0", "pd1"), ("px", "pmt", "pz", "py"))))
 
-    def part_of(part):
-        lo = 32 * "tab".index(part)
-        return lo, slice(16 * lo, 16 * lo + A)
+    def span(parts):
+        lo, n = 32 * "tab".index(parts[0]), 32 * len(parts)
+        return lo, n, slice(16 * lo, 16 * (lo + n))
 
-    def gather_methods(tl, key, part):
-        lo, c = part_of(part)
-        cp([key, "MT"], ["MG" + part], T.MG[:, c], T.MT[:, :].indirect(tl[:, lo:lo + 32]))
-
-    def method_lists(part):
-        lo, bk = part_of(part)[0], LB[part]
-        mm(["MG" + part, "ZM0", "ZM1"], [bk],
-           *[[(piece(T[bk], j), sel(z, q), T.MG[:, 16 * lo + q:16 * lo + A:16]) for q in range(16)]
-             for j, z in enumerate((T.ZM0, T.ZM1))])
-
-    def method_offsets(part):
-        lo, bk = part_of(part)[0], LB[part]
-        for j in (1, 0):
-            cp([bk], ["MU%d%s" % (j, part)], T.MU[:, 96 * j + lo:96 * j + lo + 32], piece(T[bk], j))
-
-    def vote0(part):
-        lo, c = part_of(part)
-        tt(["MU0" + part, "PC", "SB"], ["B0" + part], T.B0[:, c], T.PC[:, :].indirect(T.MU[:, lo:lo + 32]), T.SB[:, c], ALU.is_le)
-
-    def cond1(part):
-        lo, c = part_of(part)
-        act(["MU1" + part, "PC"], ["P1" + part], T.P1[:, c], T.PC[:, :].indirect(T.MU[:, 96 + lo:96 + lo + 32]), ACT.Copy)
-
-    def diff1(part):
-        lo, c = part_of(part)
-        k = lo // 32
-        mm(["SB", "P1" + part, "NI", "ID"], ["pd%d" % k], [(PD[k][:], T.NI[:], T.SB[:, c]), (PD[k][:], T.ID[:], T.P1[:, c])])
-
-    def vote1(part):
-        lo, c = part_of(part)
-        act(["pd%d" % (lo // 32), "half"], ["B1" + part], T.B1[:, c], PD[lo // 32][:], ACT.Sign, bias=T.CC[:, 31:32], scale=-1.0)
-
-    def votes(parts, j):
-        lo, n = part_of(parts[0])[0], 32 * len(parts)
-        b, z, zk = ((T.B0, T.ZN, "ZN"), (T.B1, T.ZO, "ZO"))[j]
-        mm(["B%d%s" % (j, p) for p in parts] + [zk], ["px"],
-           [(T.px[:, lo:lo + n], sel(z, q), b[:, 16 * lo + q:16 * (lo + n):16]) for q in range(16)], first=j == 0, last=j == 1)
-
-    def row_list(rnd, part):
-        lo, n, bank, bk, zt, lt, k = (0, 64, T.pz, "pz", T.ZT, T.LT, "Z") if part == "h" else (64, 32, T.pmt, "pmt", T.YT, T.LY, "Y")
-        win, items = WN[rnd % 2], []
-        for q in range(16):
-            items.append((bank[:, 0:n], sel(zt, q) if q < 13 else wide(lt, 2 * (q - 13)), win[:, 16 * (lo + 1) + q:16 * (lo + n + 1):16]))
-        for q in (13, 14, 15):
-            items.append((bank[:, 0:n], wide(lt, 2 * (q - 13) + 1), win[:, 16 * lo + q:16 * (lo + n):16]))
-        mm(["W%d" % (rnd % 2), k + "T"] + ["%s%s%d" % (k, x, q) for x in "ab" for q in (13, 14, 15)], [bk], items)
+    def stage(s):
+        lo, n = span(s)[0] // 2, 16 * len(s)
+        a = 32 * lo + (16 if lo else 0)
+        return lo, n, a, a + 16 * n + 16
 
     def row_types(rnd, part):
         lo, n, bank, bk = (32, 64, T.pz, "pz") if part == "h" else (0, 32, T.pmt, "pmt")
         ts([bk], ["TL%s%d" % (part, rnd + 1)], TL[rnd + 1][:, lo:lo + n], bank[:, 0:n], -64.0, ALU.mult, float(EMPTY), ALU.add)
 
-    GA, GB = T.G2[:, 0:NP], T.G2[:, GBO:GBO + NP]
-    for rnd in range(RO):
-        tl, win = TL[rnd], WN[rnd % 2]
+    def step(rnd, k, s):
+        tl, last, win, wk = TL[rnd], rnd == RO - 1, WN[rnd % 2], "W%d" % (rnd % 2)
         kt, kh = "TLt%d" % rnd, "TLh%d" % rnd
-        last = rnd == RO - 1
-
-        gather_methods(tl, kh, "a")
-        if rnd > 0:
-            row_types(rnd - 1, "t")
-        if last:
+        if k in "gloOcdvw01mM":
+            lo, n, c = span(s)
+        if k in "pqAGfknKjsuUW":
+            lo, n, a, b = stage(s)
+            c, k0 = slice(lo, lo + n), 16 * lo + (2 if lo else 0)
+        if k == "r" and rnd > 0:
+            row_types(rnd - 1, s)
+        if k == "x" and last:
             exchange_out("b", "y", [kt, kh], tl)
-            exchange_in("b", "y", ["TR"], T.TR)
-        act([kh, "EF"], ["Eh", "SMh"], T.EB[:, A + 1:V + 1], T.EF[:, :].indirect(tl[:, 32:96]), ACT.Copy, accum_out=T.SM[:, 0:1])
-        act([kt, "EF"], ["Et", "SMt"], T.EB[:, 1:A + 1], T.EF[:, :].indirect(tl[:, 0:32]), ACT.Copy, accum_out=T.SM[:, 1:2])
-        method_lists("a")
-        gather_methods(tl, kh, "b")
-        method_lists("b")
-        method_offsets("a")
-        gather_methods(tl, kt, "t")
-        for bank, bk in ((T.pz, "pz"), (T.pmt, "pmt"))[:2 if last else 1]:
-            mm(["SMh", "SMt", "LOW"], [bk], [(bank[:, 128:129], T.LOW[:], T.SM[:, j:j + 1]) for j in range(2)])
-        method_lists("t")
-        method_offsets("b")
-        if rnd == 0:
-            fill(["half"], T.CC[:, 31:32], 0.5)
-            fill(["XB0"], T.XB[:], 0.0)
-            fill(["EY0"], T.EY[:, 0:1], 0.0)
-        scan(["Eh", "Et", "E0", "ZW", "pz"], ["SB"], T.SB[:], T.EB[:, 0:V], T.ZW[:], T.pz[:, 128:129], ALU.add, ALU.add)
-        method_offsets("t")
-        cond1("a")
-        if last:
-            act(["pmt", "XB0"], ["XB"], T.XB[:, 0:1], T.pmt[:, 128:129], ACT.Copy)
-            exchange_out("c", "y", ["XB"], T.XB)
-            exchange_in("c", "y", ["XR"], T.XR)
-        for p in "abt":
-            vote0(p)
-        diff1("a")
-        cond1("b")
-        diff1("b")
-        cond1("t")
-        diff1("t")
-        for p in "abt":
-            vote1(p)
-        votes("ab", 0)
-        votes("ab", 1)
-        votes("t", 0)
-        votes("t", 1)
-        ts(["MU1t", "MU1a", "MU1b"], ["MF"], T.MF[:], T.MU[:, 96:192], -2048.0, ALU.add)
-        ts(["MU0t", "MU0a", "MU0b"], ["pmh"], T.pmh[:, 1:192:2], T.MU[:, 0:96], -2048.0, ALU.add)
-        if rnd == 0:
+        if k == "E":
+            lo, n, j = (32, 64, 0) if s == "h" else (0, 32, 1)
+            act(["TL%s%d" % (s, rnd), "EF"], ["E" + s, "SM" + s], T.EB[:, 16 * lo + 1:16 * (lo + n) + 1],
+                T.EF[:, :].indirect(tl[:, lo:lo + n]), ACT.Copy, accum_out=T.SM[:, j:j + 1])
+        if k == "B":
+            for bk in ("pz", "pmh")[:2 if last else 1]:
+                mm(["SMh", "SMt", "LOW"], [bk], [(T[bk][:, 128:129], T.LOW[:], T.SM[:, j:j + 1]) for j in range(2)])
+            if last:
+                act(["pmh", "XB0"], ["XB"], T.XB[:, 0:1], T.pmh[:, 128:129], ACT.Copy)
+                exchange_out("c", "y", ["XB"], T.XB)
+                exchange_in("b", "y", ["TR"], T.TR)
+                exchange_in("c", "y", ["XR"], T.XR)
+        if k == "S":
+            scan(["Eh", "Et", "E0", "ZW", "pz"], ["SB"], T.SB[:], T.EB[:, 0:V], T.ZW[:], T.pz[:, 128:129], ALU.add, ALU.add)
+        if k == "g":
+            cp([kt if s == "t" else kh, "MT"], ["MG" + s], T.MG[:, c], T.MT[:, :].indirect(tl[:, lo:lo + n]))
+        if k == "l":
+            mm(["MG" + p for p in s] + ["ZM0", "ZM1"], [LB[s[0]]],
+               *[[(T[LB[s[0]]][:, n * j:n * j + n], sel(z, q), T.MG[:, 16 * lo + q:16 * (lo + n):16]) for q in range(16)]
+                 for j, z in enumerate((T.ZM0, T.ZM1))])
+        if k in "oO":
+            j = "Oo".index(k)
+            cp([LB[s[0]]], ["MU%d%s" % (j, p) for p in s], T.MU[:, 96 * j + lo:96 * j + lo + n], T[LB[s[0]]][:, n * j:n * j + n])
+        if k == "v":
+            tt(["MU0" + s, "PC", "SB"], ["B0" + s], T.B0[:, c], T.PC[:, :].indirect(T.MU[:, lo:lo + n]), T.SB[:, c], ALU.is_le)
+        if k == "c":
+            act(["MU1" + s, "PC"], ["P1" + s], T.P1[:, c], T.PC[:, :].indirect(T.MU[:, 96 + lo:96 + lo + n]), ACT.Copy)
+        if k == "d":
+            p = PD[lo // 32]
+            mm(["SB", "P1" + s, "NI", "ID"], ["pd%d" % (lo // 32)], [(p[:], T.NI[:], T.SB[:, c]), (p[:], T.ID[:], T.P1[:, c])])
+        if k == "w":
+            act(["pd%d" % (lo // 32), "half"], ["B1" + s], T.B1[:, c], PD[lo // 32][:], ACT.Sign, bias=C["half"], scale=-1.0)
+        if k in "01":
+            bk = BK[s][0]
+            bb, z, zk = ((T.B0, T.ZN, "ZN"), (T.B1, T.ZO, "ZO"))[int(k)]
+            mm(["B%s%s" % (k, p) for p in s] + [zk], [bk if k == "0" else "VV"],
+               [(T[bk][:, 0:n], sel(z, q), bb[:, 16 * lo + q:16 * (lo + n):16]) for q in range(16)], first=k == "0", last=k == "1")
+            if k == "1":
+                writer[bk] = writer.pop("VV")
+        if k == "D":
+            ts(["MU1t", "MU1a", "MU1b"], ["MF"], T.MF[:], T.MU[:, 96:192], -2048.0, ALU.add)
+            ts(["MU0t", "MU0a", "MU0b"], ["pmh"], T.pmh[:, 1:192:2], T.MU[:, 0:96], -2048.0, ALU.add)
+        if k == "F":
+            tt(["MF", "pmh"], ["DM"], T.pmh[:, 0:192:2], T.MF[:], T.pmh[:, 1:192:2], ALU.subtract)
+        if k == "L" and rnd == 0:
             late_constants()
-        tt(["MF", "pmh"], ["DM"], T.pmh[:, 0:192:2], T.MF[:], T.pmh[:, 1:192:2], ALU.subtract)
-        if last:
-            act(["TR", "EA"], ["EYa"], T.EY[:, 1:NP + 1], T.EA[:, :].indirect(T.TR[:, 0:48]), ACT.Copy)
-
-        ts(["px"], ["VT"], T.VT[:, 1:192:2], T.px[:, 0:96], -16.0, ALU.is_gt)
-        scan(["VT", "DM", "pmh"], ["MS"], T.MS[:], T.VT[:], T.pmh[:, 0:192], 0.0, ALU.mult, ALU.add)
-        mm(["MS", "PA", "PB"], ["py"], *[[(T.py[:, 48 * j:48 * j + 48], z[:, 8:136], T.MS[:, 1:192:4]),
-                                          (T.py[:, 48 * j:48 * j + 48], z[:, 0:128], T.MS[:, 3:192:4])] for j, z in enumerate((T.PA, T.PB))])
-        if rnd == 0:
-            selectors(0)
-        ts(["py"], ["AB"], T.AB[:], T.py[:, 0:96], 2048.0, ALU.add)
-        if rnd == 0:
-            selectors(1)
-        act(["AB", "TT", "sa", "ba"], ["GA"], GA, T.TT[:, :].indirect(T.AB[:, 0:48]), ACT.Identity, scale=C["sa"], bias=C["ba"])
-        ts(["AB", "TT", "hib", "lob"], ["GB"], GB, T.TT[:, :].indirect(T.AB[:, 48:96]), C["hib"], ALU.min, C["lob"], ALU.max)
-        if last:
-            act(["TR", "EA"], ["EYb"], T.EY[:, NP + 1:V + 1], T.EA[:, :].indirect(T.TR[:, 48:96]), ACT.Copy)
-
-        mm(["GA", "GB", "G0", "ZE"], ["px"], [(T.px[:, 0:97], sel(T.ZE, q), T.G2[:, q:GBO + NP:16]) for q in range(16)])
-        scan(["GA", "GB", "G0"], ["KS"], T.KS[:, 0:NP + 1], T.G2[:, 0:NP + 1], T.G2[:, GBO - 1:GBO + NP], -float(KEY0), ALU.add, ALU.add)
-        mm(["KS", "ZA", "ZB", "ZC"], ["py"],
-           [(T.py[:, 0:48], sel(T.ZA if q == 0 else T.ZB if q == 16 else T.ZC, q), T.KS[:, q:q + NP - 15:16]) for q in range(17)])
-        if rnd == 0:
-            selectors(2)
-        tt(["px", "CD"], ["CE0"], T.CE0[:], T.px[:, 0:48], T.CD[:], ALU.add)
-        tt(["px", "CE0"], ["CE"], T.CE[:], T.px[:, 49:97], T.CE0[:], ALU.add)
-        tt(["py", "CE"], ["OF"], T.OF[:], T.py[:, 0:48], T.CE[:], ALU.max)
-        ts(["OF"], ["OU"], T.OU[:], T.OF[:], float(KEYADD), ALU.add)
-        tt(["OU", "GA", "GB"], ["W%d" % (rnd % 2)], win[:, :].indirect(T.OU[:]), GA, GB, ALU.mult)
-
-        row_list(rnd, "h")
-        row_list(rnd, "t")
-        if rnd == 0:
+        if k == "Z" and rnd == 0:
+            selectors(s)
+        if k == "m":
+            ts([BK[s][0], "VT"], ["VT" + s], T.VT[:, 2 * lo + 1:2 * (lo + n):2], T[BK[s][0]][:, 0:n], -16.0, ALU.is_gt)
+        if k == "M":
+            c = slice(2 * lo, 2 * (lo + n))
+            scan(["VT" + s, "DM", "pmh"], ["MS" + s], T.MS[:, c], T.VT[:, c], T.pmh[:, c], 0.0, ALU.mult, ALU.add)
+        if k == "p":
+            bk = BK[s][1]
+            mm(["MS" + s, "PA", "PB"], [bk], *[[(T[bk][:, n * j:n * j + n], z[:, 8:136], T.MS[:, 4 * lo + 1:4 * (lo + n):4]),
+                                               (T[bk][:, n * j:n * j + n], z[:, 0:128], T.MS[:, 4 * lo + 3:4 * (lo + n):4])]
+                                              for j, z in enumerate((T.PA, T.PB))])
+        if k == "q":
+            ts([BK[s][1]], ["AB" + s], T.AB[:, 2 * lo:2 * (lo + n)], T[BK[s][1]][:, 0:2 * n], 2048.0, ALU.add)
+        if k == "A":
+            act(["AB" + s, "TT", "sa", "ba"], ["GA" + s], T.G2[:, a:a + 16 * n], T.TT[:, :].indirect(T.AB[:, 2 * lo:2 * lo + n]),
+                ACT.Identity, scale=C["sa"], bias=C["ba"])
+        if k == "G":
+            ts(["AB" + s, "TT", "hib", "lob"], ["GB" + s], T.G2[:, b:b + 16 * n],
+               T.TT[:, :].indirect(T.AB[:, 2 * lo + n:2 * (lo + n)]), C["hib"], ALU.min, C["lob"], ALU.max)
+        if k == "f":
+            mm(["GA" + s, "GB" + s, "G0" + s, "ZE"], [BK[s][2]],
+               [(T[BK[s][2]][:, 0:2 * n + 1], sel(T.ZE, q), T.G2[:, a + q:b + 16 * n:16]) for q in range(16)])
+        if k == "k":
+            scan(["GA" + s, "GB" + s, "G0" + s] + (["KE"] if lo else []), ["KS" + s], T.KS[:, k0:k0 + 16 * n + 1],
+                 T.G2[:, a:a + 16 * n + 1], T.G2[:, b - 1:b + 16 * n], T.KE[:, 0:1] if lo else -float(KEY0), ALU.add, ALU.add)
+        if k == "n":
+            mm(["KS" + s, "ZA", "ZB", "ZC"], [BK[s][3]],
+               [(T[BK[s][3]][:, 0:n], sel(T.ZA if q == 0 else T.ZB if q == 16 else T.ZC, q),
+                 T.KS[:, k0 + q:k0 + q + 16 * n - 15:16]) for q in range(17)])
+        if k == "K":
+            cp(["KS" + s], ["KE"], T.KE[:, 0:1], T.KS[:, 16 * n:16 * n + 1])
+        if k == "j":
+            tt([BK[s][2], "CD"], ["CE0" + s], T.CE0[:, c], T[BK[s][2]][:, 0:n], T.CD[:, c], ALU.add)
+        if k == "s":
+            tt([BK[s][2], "CE0" + s], ["CE" + s], T.CE[:, c], T[BK[s][2]][:, n + 1:2 * n + 1], T.CE0[:, c], ALU.add)
+        if k == "u":
+            tt([BK[s][3], "CE" + s], ["OF" + s], T.OF[:, c], T[BK[s][3]][:, 0:n], T.CE[:, c], ALU.max)
+        if k == "U":
+            ts(["OF" + s], ["OU" + s], T.OU[:, c], T.OF[:, c], float(KEYADD), ALU.add)
+        if k == "W":
+            tt(["OU" + s, "GA" + s, "GB" + s], [wk], win[:, :].indirect(T.OU[:, c]),
+               T.G2[:, a:a + 16 * n], T.G2[:, b:b + 16 * n], ALU.mult)
+        if k == "R":
+            lo, n, bk, zt, lt, z = (0, 64, "pz", T.ZT, T.LT, "Z") if s == "h" else (64, 32, "pmt", T.YT, T.LY, "Y")
+            o = T[bk][:, 0:n]
+            items = [(o, sel(zt, q) if q < 13 else wide(lt, 2 * (q - 13)), win[:, 16 * (lo + 1) + q:16 * (lo + n + 1):16])
+                     for q in range(16)]
+            items += [(o, wide(lt, 2 * (q - 13) + 1), win[:, 16 * lo + q:16 * (lo + n):16]) for q in (13, 14, 15)]
+            mm([wk, z + "T"] + ["%s%s%d" % (z, x, q) for x in "ab" for q in (13, 14, 15)], [bk], items)
+        if k == "C" and rnd == 0:
             clear(0)
-        if not last:
-            row_types(rnd, "h")
+        if k == "y" and last:
+            lo = 48 * "ab".index(s)
+            act(["TR", "EA"], ["EY" + s], T.EY[:, 16 * lo + 1:16 * lo + NP + 1], T.EA[:, :].indirect(T.TR[:, lo:lo + 48]), ACT.Copy)
+        if k == "Y" and last:
+            scan(["EYa", "EY0", "ZW", "XR"], ["YSa"], T.YS[:, 0:NP], T.EY[:, 0:NP], T.ZW[:, 0:NP], T.XR[:, 0:1], ALU.add, ALU.add)
+            dmas("s", "dys0", ["YSa"], [], [(T.ys[:, 0:NP], T.YS[:, 0:NP])])
 
-    scan(["EYa", "EY0", "ZW", "XR"], ["YSa"], T.YS[:, 0:NP], T.EY[:, 0:NP], T.ZW[:, 0:NP], T.XR[:, 0:1], ALU.add, ALU.add)
-    dmas("s", "dys0", ["YSa"], [], [(T.ys[:, 0:NP], T.YS[:, 0:NP])])
-    row_types(RO - 1, "h")
+    for rnd in range(RO):
+        for w in ORDER.split():
+            step(rnd, w[0], w[1:])
+
     row_types(RO - 1, "t")
+    row_types(RO - 1, "h")
     exchange_out("d", "y", ["TLh%d" % RO, "TLt%d" % RO], T.YP)
     scan(["EYa", "EYb", "ZW", "YSa"], ["YSb"], T.YS[:, NP:V], T.EY[:, NP:V], T.ZW[:, 0:NP], T.YS[:, NP - 1:NP], ALU.add, ALU.add)
-    dmas("s", "dys1", ["YSb"], [], [(T.ys[:, NP:V], T.YS[:, NP:V])])
+    dmas("y", "dys1", ["YSb"], [], [(T.ys[:, NP:V], T.YS[:, NP:V])])
     exchange_in("d", "y", [], T.yp)
     wait("y", list(count.items()))

from concourse.bass import DstId, RemoteDMATransfer
from concourse.mybir import AluOpType, ActivationFunctionType

ALU = AluOpType
ACT = ActivationFunctionType
N, V, A, W, M, RO = 8, 1536, 512, 3072, 4096, 3
H = V - A
EMPTY = W - 1
NP = V // 2
WREAD = V + 16
WDUMMY = 2 * V + 16
WCOLS = WDUMMY + NP
KEY0 = 1024
KEYADD = KEY0 + 13
RND = 12582912.0
F32, BF, F16, I32, U16 = "float32", "bfloat16", "float16", "int32", "uint16"
STAGES = ("ta", "b")
ORDER = ("rt gt Et rh Eh lt ga gb ot ct la Ot Z1 Oa x B oa ca S lb Ob ob cb va dt wt vt da wa vb D L db 0ta F 1ta mta Mta Z0 0b wb 1b mb pta qta Ata Mb Gta pb qb kta Ab fta Gb Kta ya nta jta Z2 sta kb yb uta fb jb Uta sb Wta nb ub Ub Wb Y Rt Rh C")

SCRATCH = {k: ("sbuf", [128, n], d) for d, names in (
    (I32, dict(TD=96, KC=128, K2=256, MC=96, M2=96, CI=4)),
    (BF, dict(MD=96, DG=128, ST=512, ZS=64, O1=512, EF=W, EA=W, PC=M, MT=W, TT=M, IX=160, IM=128,
              ZO=144, ZN=144, ZM0=144, ZM1=144, Z1=148, Z2=148, ZT=148, Y1=148, Y2=148, YT=148, LT=768, LY=768,
              ZA=144, ZB=144, ZC=144, ZE=144, PA=136, PB=136,
              ID=128, NI=128, ZW=V, EB=V + 2, EY=V + 2, MG=V, P1=V, B0=V, B1=V, SB=V, G2=V + 32,
              W0=WCOLS, W1=WCOLS)),
    (F32, dict(CF=4, CX=48, CD=48, CC=32, TG=8, TG0=8, TI=2, TI0=2, YP=96, YS=V, MF=96, VT=192,
               CE=48, CE0=48, OF=48, SM=2, UF=256, IF=32, L1=128, LOW=128, XB=16, XR=16, KE=2)),
    (F16, dict(MS=192, KS=NP + 4)),
    (U16, dict(TL0=96, TL1=96, TL2=96, TR=96, MU=192, AB=96, OU=48)),
) for k, n in names.items()}
PSUM_KEYS = ("pd0", "pd1", "pd2", "pmh", "pmt", "px", "py", "pz")
SCRATCH.update({k: ("psum", [128, 512], F32) for k in PSUM_KEYS})
EXCH = dict(a=(12, I32), b=(12, U16), c=(2, F32), d=(12, F32))
for _k, (_n, _d) in EXCH.items():
    SCRATCH["DO" + _k] = ("dram", [N, 128, _n], _d)
    SCRATCH["DI" + _k] = ("dram", [N, 128, _n], _d)
SEMAPHORES = (["cv", "cs", "ct", "cg", "sent", "dkc", "dmc", "def", "dpc", "dmt", "dtt", "dea", "dys0", "dys1"]
              + [p + k for k in EXCH for p in ("xo", "xs", "xr", "xi")])


def rank_program(g, core, T, topo):
    rank = T.rank_of(core)
    if rank is None:
        return
    cores = T.cores
    Q = {"v": g.vector, "s": g.scalar, "t": g.tensor, "g": g, "y": g.sync}
    own = {"v": "cv", "s": "cs", "t": "ct", "g": "cg"}
    count = {}
    seen = {q: {} for q in Q}
    writer, readers = {}, {}

    def wait(q, toks):
        need = {}
        for s, v in toks:
            if v > seen[q].get(s, 0) and v > need.get(s, 0):
                need[s] = v
        for s, v in need.items():
            Q[q].wait_ge(T.sem[s], v)
            seen[q][s] = v

    def before(q, rd, wr):
        toks = []
        for k in rd:
            toks += writer.get(k, [])
            if k in PSUM_KEYS:
                toks += [t for t in readers.get(k, []) if t[0] != own.get(q)]
        for k in wr:
            toks += writer.get(k, []) + readers.get(k, [])
        wait(q, toks)

    def after(tok, rd, wr):
        for k in rd:
            readers.setdefault(k, []).append(tok)
        for k in wr:
            writer[k] = [tok]
            readers[k] = []

    def op(q, rd, wr, fn):
        before(q, rd, wr)
        s = own[q]
        fn().then_inc(T.sem[s], 1)
        count[s] = count.get(s, 0) + 1
        after((s, count[s]), rd, wr)

    def dmas(q, s, rd, wr, pairs):
        before(q, rd, wr)
        for o, i in pairs:
            Q[q].dma_start(o, i).then_inc(T.sem[s], 16)
        count[s] = count.get(s, 0) + 16 * len(pairs)
        after((s, count[s]), rd, wr)

    def mm(rd, wr, *groups, first=True, last=True):
        def run():
            for items in groups:
                for n, (o, l, r) in enumerate(items):
                    ins = g.tensor.matmul(o, l, r, first and n == 0, last and n == len(items) - 1)
            return ins
        op("t", rd, wr, run)

    def ts(rd, wr, out, in0, s1, op0, s2=None, op1=None):
        if op1 is None:
            op("v", rd, wr, lambda: g.vector.tensor_scalar(out, in0, s1, None, op0))
        else:
            op("v", rd, wr, lambda: g.vector.tensor_scalar(out, in0, s1, s2, op0, op1))

    def tt(rd, wr, out, in0, in1, o):
        op("v", rd, wr, lambda: g.vector.tensor_tensor(out, in0, in1, o))

    def cp(rd, wr, out, in_):
        op("v", rd, wr, lambda: g.vector.tensor_copy(out, in_))

    def fill(wr, ap, c):
        op("v", [], wr, lambda: g.vector.memset(ap, c))

    def scan(rd, wr, out, d0, d1, init, o0, o1):
        op("v", rd, wr, lambda: g.vector.tensor_tensor_scan(out, d0, d1, init, o0, o1))

    def act(rd, wr, out, in_, f, **kw):
        op("s", rd, wr, lambda: g.scalar.activation(out, in_, f, **kw))

    def iota(wr, out, pattern, base):
        op("g", [], wr, lambda: g.iota(out, pattern, base, 0, allow_small_or_imprecise_dtypes=True))

    others = [r for r in range(N) if r != rank]
    away = [r for r in others if topo.chip(cores[r]) != topo.chip(core)]
    far = topo.engines(core, cores[away[0]])
    engine = {r: far[n] for n, r in enumerate(away)}
    for r in others:
        if r not in engine:
            engine[r] = next(e for e in topo.engines(core, cores[r]) if e not in far and e not in engine.values())
    mine = slice(16 * rank, 16 * rank + 16)

    def exchange_out(k, q, rd, src):
        DO, DI = T["DO" + k], T["DI" + k]
        dmas(q, "xo" + k, rd, ["DO" + k], [(DO[:], src[:])])
        dmas(q, "xs" + k, rd, ["DS" + k], [(DI[rank], src[mine, :])])
        before("g", ["DO" + k], [])
        g.remote_dma_fused([RemoteDMATransfer(dst_ids=[DstId(rid=topo.addr(cores[r])[0], pnc=topo.addr(cores[r])[1])],
                                              dma_engine_mask=1 << engine[r], remote_sem=T.sem["xr" + k],
                                              src=DO[r], dst=DI[rank]) for r in others], local_sem=T.sem["sent"])
        count["sent"] = count.get("sent", 0) + len(others)
        count["xr" + k] = len(others)
        writer["DR" + k] = [("xr" + k, len(others))]

    def exchange_in(k, q, wr, dst):
        dmas(q, "xi" + k, ["DS" + k, "DR" + k], wr, [(dst[:], T["DI" + k][:])])

    def groups(dst, src):
        return [(dst[16 * j:16 * j + 16, :], src) for j in range(N)]

    TL = [T.TL0, T.TL1, T.TL2, T.YP]
    WN = [T.W0, T.W1]
    PD = [T.pd0, T.pd1, T.pd2]

    op("g", [], ["CI0"], lambda: g.iota(T.CI[:, 0:1], [[1, 1]], 0, 1))
    iota(["IX"], T.IX[:], [[1, 160]], 0)
    iota(["IM"], T.IM[:], [[0, 8], [1, 16]], 0)
    exchange_out("a", "y", [], T.todo)
    dmas("s", "dmc", [], [], [(T.MC[32 * j:32 * j + 32, :], T.meth[rank, :]) for j in (0, 1)])
    dmas("y", "dmc", [], ["MC"], [(T.MC[32 * j:32 * j + 32, :], T.meth[rank, :]) for j in (2, 3)])
    dmas("s", "dkc", [], ["KC"], [(T.KC[0:32, :], T.kid[rank, :])])
    dmas("y", "def", [], ["EF"], groups(T.EF, T.eff[mine, :]))

    fill(["MT"], T.MT[:], 0.0)
    ts(["CI0"], ["CI1"], T.CI[:, 1:2], T.CI[:, 0:1], 15, ALU.bitwise_and)
    ts(["CI0"], ["CI2"], T.CI[:, 2:3], T.CI[:, 0:1], 112, ALU.bitwise_and)
    ts(["CI0"], ["CI3"], T.CI[:, 3:4], T.CI[:, 0:1], 15, ALU.bitwise_and, 1, ALU.logical_shift_right)

    ts(["MC"], ["M2a"], T.M2[0:32, :], T.MC[0:32, :], 4095 - 63, ALU.bitwise_and)
    ts(["MC"], ["M2b"], T.M2[32:64, :], T.MC[32:64, :], 63, ALU.bitwise_and)
    ts(["MC"], ["M2c"], T.M2[64:96, :], T.MC[64:96, :], 12, ALU.logical_shift_right, 4095 - 63, ALU.bitwise_and)
    ts(["MC"], ["M2d"], T.M2[96:128, :], T.MC[96:128, :], 12, ALU.logical_shift_right, 63, ALU.bitwise_and)
    cp(["CI0", "CI1", "CI2", "CI3"], ["CF"], T.CF[:], T.CI[:])
    cp(["M2a", "M2b", "M2c", "M2d"], ["MD"], T.MD[:], T.M2[:])
    dmas("s", "dmt", ["MD"], ["MT"], [(T.MT[16 * j:16 * j + 4, :], T.MD[:]) for j in range(N)])
    exchange_in("a", "y", ["TD"], T.TD)
    dmas("y", "dpc", [], ["PC"], groups(T.PC, T.pre[mine, :]))

    kc, ic, gcol, hc = T.CF[:, 0:1], T.CF[:, 1:2], T.CF[:, 2:3], T.CF[:, 3:4]
    names = "b16 od sg hb ta t1 g2 g4 g6 r0 r1 tz ty g7 w1 w2 wa ba sa e6 x0 y0 hib lob half".split()
    C = {k: T.CC[:, j:j + 1] for j, k in enumerate(names)}

    def col(k, rd, in0, s1, op0, s2=None, op1=None):
        ts(["CF"] + rd, [k], C[k], in0, s1, op0, s2, op1)

    def piece(b, j, n=1):
        return b[:, 32 * j:32 * (j + n)]

    def row(i):
        return piece(T.ST, i)

    def wide(b, j):
        return b[:, 128 * j:128 * j + 128]

    ts(["KC"], ["K2a"], T.K2[0:32, 0:128], T.KC[0:32, :], 4095, ALU.bitwise_and)
    ts(["KC"], ["K2b"], T.K2[0:32, 128:256], T.KC[0:32, :], 12, ALU.logical_shift_right)
    ts(["CF", "IX"], ["IF"], T.IF[:], T.IX[:, 0:32], kc, ALU.is_equal)
    ts(["CF", "IM"], ["L1"], T.L1[:], T.IM[:], ic, ALU.is_equal)
    ts(["K2a", "K2b"], ["UF"], T.UF[0:32, :], T.K2[0:32, :], -1.0 / 64, ALU.mult, EMPTY / 64.0, ALU.add)
    mm(["UF", "IF"], ["pd0"], *[[(piece(T.pd0, j), T.UF[0:32, 128 * j:128 * j + 128], T.IF[0:32, :])] for j in range(2)])
    op("g", ["L1"], ["LOW"], lambda: g.affine_select(T.LOW[:], T.L1[:], [[1, 128]], ALU.is_gt, 0.0, 0, -1))
    iota(["ZW"], T.ZW[:], [[0, V]], 0)
    iota(["CX"], T.CX[:], [[16, 48]], WDUMMY - KEYADD)

    def clear(w):
        iota(["W%d" % w], WN[w][:, 0:WREAD], [[0, WREAD]], 0)

    clear(0)
    ts(["CF", "IX"], ["ID"], T.ID[:], T.IX[:, 0:128], kc, ALU.is_equal)
    ts(["CF", "IX"], ["NI"], T.NI[:], T.IX[:, 0:128], kc, ALU.is_equal, -1.0, ALU.mult)
    col("b16", [], gcol, 16.0, ALU.add)
    ts(["CF", "IX"], ["TG0"], T.TG0[:], T.IX[:, 0:8], hc, ALU.subtract, 1000.0, ALU.mult)
    fill(["ST14"], piece(T.ST, 14, 2), 0.0)
    ts(["pd0"], ["DGh"], T.DG[:, 0:64], T.pd0[:, 0:64], RND, ALU.add, RND, ALU.subtract)
    ts(["pd0"], ["pd1"], T.pd1[:, 0:64], T.pd0[:, 0:64], 0.0, ALU.is_gt)
    ts(["pd0"], ["ZS"], T.ZS[:], T.pd0[:, 0:64], 0.0, ALU.is_gt)
    ts(["TG0", "b16"], ["TG"], T.TG[:], T.TG0[:], C["b16"], ALU.add)
    tt(["pd0", "DGh"], ["DGl"], T.DG[:, 64:128], T.DG[:, 0:64], T.pd0[:, 0:64], ALU.subtract)
    tt(["pd1", "ZS"], ["ST12"], row(12), piece(T.pd1, 0), piece(T.ZS, 1), ALU.add)
    tt(["pd1", "ZS"], ["ST13"], row(13), piece(T.pd1, 0), piece(T.ZS, 1), ALU.max)
    for i, z, d in ((0, 1, 0), (6, 0, 1), (1, 1, 2), (7, 0, 3)):
        tt(["pd1", "DGh", "DGl"], ["ST%d" % i], row(i), piece(T.pd1, z), piece(T.DG, d), ALU.mult)

    def both(o, j, i):
        return [(o, T.ID[:], piece(T.DG, j)), (o, T.ID[:], piece(T.DG, j + 1)), (o, T.NI[:], row(i))]

    def plus(o, i):
        return [(o, T.ID[:], row(i))]

    kk = ["DGh", "DGl", "ST0", "ST1", "ST6", "ST7", "ST13", "ID", "NI"]
    mm(kk, ["pd2"], *[both(piece(T.pd2, j), d, i) for j, (d, i) in enumerate(((0, 0), (2, 1), (0, 6), (2, 7)))])
    mm(kk, ["px"], *([plus(piece(T.px, j), j) + plus(piece(T.px, j), 13) for j in range(2)]
                     + [both(piece(T.px, 2 + j), 2 * j, j) + plus(piece(T.px, 2 + j), 13) for j in range(2)]))
    act(["pd2"], ["ST2"], piece(T.ST, 2, 4), piece(T.pd2, 0, 4), ACT.Copy)
    act(["px"], ["ST8"], piece(T.ST, 8, 4), piece(T.px, 0, 4), ACT.Copy)
    mm(kk + ["ST2", "ST8", "ST12", "ST14"], ["pmt"], *[[(wide(T.pmt, b), T.ST[:, b:512:4], T.ID[:])] for b in range(4)])
    act(["pmt"], ["O1"], T.O1[:], T.pmt[:], ACT.Copy)
    dmas("y", "dtt", ["O1"], ["TT"], groups(T.TT, T.O1[:]))
    dmas("y", "dea", ["TT"], ["EA"], [(T.EA[:], T.eff[:])])

    ts(["TG", "IX"], ["ZM0"], T.ZM0[:], T.IX[:, 0:144], T.TG[:, 0:1], ALU.is_equal)
    ts(["TG", "IX"], ["ZM1"], T.ZM1[:], T.IX[:, 0:144], T.TG[:, 1:2], ALU.is_equal)
    fill(["E0"], T.EB[:, 0:1], 0.0)
    ts(["b16", "IX"], ["ZO"], T.ZO[:], T.IX[:, 0:144], C["b16"], ALU.is_equal)
    ts(["b16", "IX"], ["ZN"], T.ZN[:], T.IX[:, 0:144], C["b16"], ALU.is_equal, -2.0, ALU.mult)

    col("od", [], hc, -2.0, ALU.mult, ic, ALU.add)
    col("hb", [], hc, gcol, ALU.add, 8.0, ALU.add)
    col("t1", [], ic, 4.0, ALU.is_lt)
    col("g2", [], hc, 2.0, ALU.is_ge)
    col("g4", [], hc, 4.0, ALU.is_ge)
    col("g6", [], hc, 6.0, ALU.is_ge)
    col("g7", [], gcol, 112.0, ALU.is_ge, -128.0, ALU.mult)
    col("wa", [], ic, -2.0, ALU.mult, 25.0, ALU.add)
    cp(["TD"], ["TLt0", "TLh0"], T.TL0[:], T.TD[:])

    def late_constants():
        col("ta", ["od", "hb"], C["od"], 1000.0, ALU.mult, C["hb"], ALU.add)
        col("ba", ["g2", "g4"], C["g2"], C["g4"], ALU.subtract)
        fill(["VT"], T.VT[:], 0.0)
        col("sg", ["od"], C["od"], -2.0, ALU.mult, 1.0, ALU.add)
        col("r0", ["g4", "g2"], C["g4"], -3.0, ALU.mult, C["g2"], ALU.subtract)
        col("r1", ["g6", "b16"], C["g6"], 1000.0, ALU.mult, C["b16"], ALU.add)
        ts(["ta", "IX"], ["PA"], T.PA[:], T.IX[:, 0:136], C["ta"], ALU.is_equal)
        ts(["ta", "IX"], ["PB"], T.PB[:], T.IX[:, 0:136], 1000.0, ALU.add, C["ta"], ALU.is_equal)
        col("w2", ["sg", "g4"], C["sg"], C["g4"], ALU.mult, 2.0, ALU.mult)
        col("e6", ["ba"], hc, 6.0, ALU.is_equal, C["ba"], ALU.add)
        col("y0", ["g4", "g6"], C["g4"], C["g6"], ALU.subtract, 0.5, ALU.mult)
        col("tz", ["r0", "r1"], C["r0"], hc, ALU.add, C["r1"], ALU.add)
        col("sa", ["ba"], ic, 13.0, ALU.is_lt, C["ba"], ALU.subtract)
        col("lob", ["ba", "t1"], C["ba"], -10000.0, ALU.mult, C["t1"], ALU.add)
        col("x0", ["e6", "t1"], C["e6"], 10000.0, ALU.mult, C["t1"], ALU.add)
        col("w1", ["w2", "sg"], C["w2"], -1.5, ALU.mult, C["sg"], ALU.add)
        col("ty", ["tz", "g7"], C["tz"], 16.0, ALU.add, C["g7"], ALU.add)
        col("hib", ["x0", "y0"], C["x0"], C["y0"], ALU.add)

    def read_selectors(z1, z2, zt, lt, t, k):
        fill([k + "1a"], z1[:, 0:1], 0.0)
        ts([t, "w1", "IX"], [k + "1"], z1[:, 1:148], T.IX[:, 0:147], C[t], ALU.is_equal, C["w1"], ALU.mult)
        ts([t, "w2", "IX"], [k + "2"], z2[:], T.IX[:, 0:148], C[t], ALU.is_equal, C["w2"], ALU.mult)
        tt([k + "1", k + "1a", k + "2"], [k + "T"], zt[:], z1[:], z2[:], ALU.add)
        for n, q in enumerate((13, 14, 15)):
            op("g", [k + "T"], [k + "a%d" % q],
               lambda: g.affine_select(wide(lt, 2 * n), zt[:, 16 - q:144 - q], [[0, 8], [1, 16]], ALU.is_ge, 0.0, -8, 0))
            op("g", [k + "T"], [k + "b%d" % q],
               lambda: g.affine_select(wide(lt, 2 * n + 1), zt[:, 32 - q:160 - q], [[0, 8], [-1, 16]], ALU.is_gt, 0.0, 8, 0))

    def selectors(step):
        if step == "0":
            read_selectors(T.Z1, T.Z2, T.ZT, T.LT, "tz", "Z")
        elif step == "1":
            ts(["CF", "IX"], ["TI0"], T.TI0[:], T.IX[:, 12:14], ic, ALU.subtract, 1000.0, ALU.mult)
            for s in STAGES:
                fill(["G0" + s], T.G2[:, stage(s)[3] - 16:stage(s)[3]], 0.0)
            ts(["TG", "wa", "IX"], ["ZA"], T.ZA[:], T.IX[:, 0:144], T.TG[:, 6:7], ALU.is_equal, C["wa"], ALU.mult)
            ts(["CF", "CX"], ["CD"], T.CD[:], T.CX[:], ic, ALU.add)
            ts(["TI0", "b16"], ["TI"], T.TI[:], T.TI0[:], C["b16"], ALU.add)
            fill(["half"], C["half"], 0.5)
            fill(["XB0"], T.XB[:], 0.0)
            fill(["EY0"], T.EY[:, 0:1], 0.0)
            ts(["TI", "IX"], ["ZB"], T.ZB[:], T.IX[:, 1:145], T.TI[:, 1:2], ALU.is_equal)
            ts(["TI", "IX"], ["ZE"], T.ZE[:], T.IX[:, 0:144], T.TI[:, 0:1], ALU.is_equal, -8192.0, ALU.mult)
            tt(["ZA", "ZB"], ["ZC"], T.ZC[:], T.ZA[:], T.ZB[:], ALU.add)
        else:
            read_selectors(T.Y1, T.Y2, T.YT, T.LY, "ty", "Y")
            clear(1)

    def sel(z, q):
        return z[:, 16 - q:144 - q]

    LB = dict(t="py", a="pmt", b="px")
    BK = dict(zip(STAGES, (("pz", "py", "pd0", "pd1"), ("px", "pmt", "pz", "py"))))

    def span(parts):
        lo, n = 32 * "tab".index(parts[0]), 32 * len(parts)
        return lo, n, slice(16 * lo, 16 * (lo + n))

    def stage(s):
        lo, n = span(s)[0] // 2, 16 * len(s)
        a = 32 * lo + (16 if lo else 0)
        return lo, n, a, a + 16 * n + 16

    def row_types(rnd, part):
        lo, n, bank, bk = (32, 64, T.pz, "pz") if part == "h" else (0, 32, T.pmt, "pmt")
        ts([bk], ["TL%s%d" % (part, rnd + 1)], TL[rnd + 1][:, lo:lo + n], bank[:, 0:n], -64.0, ALU.mult, float(EMPTY), ALU.add)

    def step(rnd, k, s):
        tl, last, win, wk = TL[rnd], rnd == RO - 1, WN[rnd % 2], "W%d" % (rnd % 2)
        kt, kh = "TLt%d" % rnd, "TLh%d" % rnd
        if k in "gloOcdvw01mM":
            lo, n, c = span(s)
        if k in "pqAGfknKjsuUW":
            lo, n, a, b = stage(s)
            c, k0 = slice(lo, lo + n), 16 * lo + (2 if lo else 0)
        if k == "r" and rnd > 0:
            row_types(rnd - 1, s)
        if k == "x" and last:
            exchange_out("b", "y", [kt, kh], tl)
        if k == "E":
            lo, n, j = (32, 64, 0) if s == "h" else (0, 32, 1)
            act(["TL%s%d" % (s, rnd), "EF"], ["E" + s, "SM" + s], T.EB[:, 16 * lo + 1:16 * (lo + n) + 1],
                T.EF[:, :].indirect(tl[:, lo:lo + n]), ACT.Copy, accum_out=T.SM[:, j:j + 1])
        if k == "B":
            for bk in ("pz", "pmh")[:2 if last else 1]:
                mm(["SMh", "SMt", "LOW"], [bk], [(T[bk][:, 128:129], T.LOW[:], T.SM[:, j:j + 1]) for j in range(2)])
            if last:
                act(["pmh", "XB0"], ["XB"], T.XB[:, 0:1], T.pmh[:, 128:129], ACT.Copy)
                exchange_out("c", "y", ["XB"], T.XB)
                exchange_in("b", "y", ["TR"], T.TR)
                exchange_in("c", "y", ["XR"], T.XR)
        if k == "S":
            scan(["Eh", "Et", "E0", "ZW", "pz"], ["SB"], T.SB[:], T.EB[:, 0:V], T.ZW[:], T.pz[:, 128:129], ALU.add, ALU.add)
        if k == "g":
            cp([kt if s == "t" else kh, "MT"], ["MG" + s], T.MG[:, c], T.MT[:, :].indirect(tl[:, lo:lo + n]))
        if k == "l":
            mm(["MG" + p for p in s] + ["ZM0", "ZM1"], [LB[s[0]]],
               *[[(T[LB[s[0]]][:, n * j:n * j + n], sel(z, q), T.MG[:, 16 * lo + q:16 * (lo + n):16]) for q in range(16)]
                 for j, z in enumerate((T.ZM0, T.ZM1))])
        if k in "oO":
            j = "Oo".index(k)
            cp([LB[s[0]]], ["MU%d%s" % (j, p) for p in s], T.MU[:, 96 * j + lo:96 * j + lo + n], T[LB[s[0]]][:, n * j:n * j + n])
        if k == "v":
            tt(["MU0" + s, "PC", "SB"], ["B0" + s], T.B0[:, c], T.PC[:, :].indirect(T.MU[:, lo:lo + n]), T.SB[:, c], ALU.is_le)
        if k == "c":
            act(["MU1" + s, "PC"], ["P1" + s], T.P1[:, c], T.PC[:, :].indirect(T.MU[:, 96 + lo:96 + lo + n]), ACT.Copy)
        if k == "d":
            p = PD[lo // 32]
            mm(["SB", "P1" + s, "NI", "ID"], ["pd%d" % (lo // 32)], [(p[:], T.NI[:], T.SB[:, c]), (p[:], T.ID[:], T.P1[:, c])])
        if k == "w":
            act(["pd%d" % (lo // 32), "half"], ["B1" + s], T.B1[:, c], PD[lo // 32][:], ACT.Sign, bias=C["half"], scale=-1.0)
        if k in "01":
            bk = BK[s][0]
            bb, z, zk = ((T.B0, T.ZN, "ZN"), (T.B1, T.ZO, "ZO"))[int(k)]
            mm(["B%s%s" % (k, p) for p in s] + [zk], [bk if k == "0" else "VV"],
               [(T[bk][:, 0:n], sel(z, q), bb[:, 16 * lo + q:16 * (lo + n):16]) for q in range(16)], first=k == "0", last=k == "1")
            if k == "1":
                writer[bk] = writer.pop("VV")
        if k == "D":
            ts(["MU1t", "MU1a", "MU1b"], ["MF"], T.MF[:], T.MU[:, 96:192], -2048.0, ALU.add)
            ts(["MU0t", "MU0a", "MU0b"], ["pmh"], T.pmh[:, 1:192:2], T.MU[:, 0:96], -2048.0, ALU.add)
        if k == "F":
            tt(["MF", "pmh"], ["DM"], T.pmh[:, 0:192:2], T.MF[:], T.pmh[:, 1:192:2], ALU.subtract)
        if k == "L" and rnd == 0:
            late_constants()
        if k == "Z" and rnd == 0:
            selectors(s)
        if k == "m":
            ts([BK[s][0], "VT"], ["VT" + s], T.VT[:, 2 * lo + 1:2 * (lo + n):2], T[BK[s][0]][:, 0:n], -16.0, ALU.is_gt)
        if k == "M":
            c = slice(2 * lo, 2 * (lo + n))
            scan(["VT" + s, "DM", "pmh"], ["MS" + s], T.MS[:, c], T.VT[:, c], T.pmh[:, c], 0.0, ALU.mult, ALU.add)
        if k == "p":
            bk = BK[s][1]
            mm(["MS" + s, "PA", "PB"], [bk], *[[(T[bk][:, n * j:n * j + n], z[:, 8:136], T.MS[:, 4 * lo + 1:4 * (lo + n):4]),
                                               (T[bk][:, n * j:n * j + n], z[:, 0:128], T.MS[:, 4 * lo + 3:4 * (lo + n):4])]
                                              for j, z in enumerate((T.PA, T.PB))])
        if k == "q":
            ts([BK[s][1]], ["AB" + s], T.AB[:, 2 * lo:2 * (lo + n)], T[BK[s][1]][:, 0:2 * n], 2048.0, ALU.add)
        if k == "A":
            act(["AB" + s, "TT", "sa", "ba"], ["GA" + s], T.G2[:, a:a + 16 * n], T.TT[:, :].indirect(T.AB[:, 2 * lo:2 * lo + n]),
                ACT.Identity, scale=C["sa"], bias=C["ba"])
        if k == "G":
            ts(["AB" + s, "TT", "hib", "lob"], ["GB" + s], T.G2[:, b:b + 16 * n],
               T.TT[:, :].indirect(T.AB[:, 2 * lo + n:2 * (lo + n)]), C["hib"], ALU.min, C["lob"], ALU.max)
        if k == "f":
            mm(["GA" + s, "GB" + s, "G0" + s, "ZE"], [BK[s][2]],
               [(T[BK[s][2]][:, 0:2 * n + 1], sel(T.ZE, q), T.G2[:, a + q:b + 16 * n:16]) for q in range(16)])
        if k == "k":
            scan(["GA" + s, "GB" + s, "G0" + s] + (["KE"] if lo else []), ["KS" + s], T.KS[:, k0:k0 + 16 * n + 1],
                 T.G2[:, a:a + 16 * n + 1], T.G2[:, b - 1:b + 16 * n], T.KE[:, 0:1] if lo else -float(KEY0), ALU.add, ALU.add)
        if k == "n":
            mm(["KS" + s, "ZA", "ZB", "ZC"], [BK[s][3]],
               [(T[BK[s][3]][:, 0:n], sel(T.ZA if q == 0 else T.ZB if q == 16 else T.ZC, q),
                 T.KS[:, k0 + q:k0 + q + 16 * n - 15:16]) for q in range(17)])
        if k == "K":
            cp(["KS" + s], ["KE"], T.KE[:, 0:1], T.KS[:, 16 * n:16 * n + 1])
        if k == "j":
            tt([BK[s][2], "CD"], ["CE0" + s], T.CE0[:, c], T[BK[s][2]][:, 0:n], T.CD[:, c], ALU.add)
        if k == "s":
            tt([BK[s][2], "CE0" + s], ["CE" + s], T.CE[:, c], T[BK[s][2]][:, n + 1:2 * n + 1], T.CE0[:, c], ALU.add)
        if k == "u":
            tt([BK[s][3], "CE" + s], ["OF" + s], T.OF[:, c], T[BK[s][3]][:, 0:n], T.CE[:, c], ALU.max)
        if k == "U":
            ts(["OF" + s], ["OU" + s], T.OU[:, c], T.OF[:, c], float(KEYADD), ALU.add)
        if k == "W":
            tt(["OU" + s, "GA" + s, "GB" + s], [wk], win[:, :].indirect(T.OU[:, c]),
               T.G2[:, a:a + 16 * n], T.G2[:, b:b + 16 * n], ALU.mult)
        if k == "R":
            lo, n, bk, zt, lt, z = (0, 64, "pz", T.ZT, T.LT, "Z") if s == "h" else (64, 32, "pmt", T.YT, T.LY, "Y")
            o = T[bk][:, 0:n]
            items = [(o, sel(zt, q) if q < 13 else wide(lt, 2 * (q - 13)), win[:, 16 * (lo + 1) + q:16 * (lo + n + 1):16])
                     for q in range(16)]
            items += [(o, wide(lt, 2 * (q - 13) + 1), win[:, 16 * lo + q:16 * (lo + n):16]) for q in (13, 14, 15)]
            mm([wk, z + "T"] + ["%s%s%d" % (z, x, q) for x in "ab" for q in (13, 14, 15)], [bk], items)
        if k == "C" and rnd == 0:
            clear(0)
        if k == "y" and last:
            lo = 48 * "ab".index(s)
            act(["TR", "EA"], ["EY" + s], T.EY[:, 16 * lo + 1:16 * lo + NP + 1], T.EA[:, :].indirect(T.TR[:, lo:lo + 48]), ACT.Copy)
        if k == "Y" and last:
            scan(["EYa", "EY0", "ZW", "XR"], ["YSa"], T.YS[:, 0:NP], T.EY[:, 0:NP], T.ZW[:, 0:NP], T.XR[:, 0:1], ALU.add, ALU.add)
            dmas("s", "dys0", ["YSa"], [], [(T.ys[:, 0:NP], T.YS[:, 0:NP])])

    for rnd in range(RO):
        for w in ORDER.split():
            step(rnd, w[0], w[1:])

    row_types(RO - 1, "t")
    row_types(RO - 1, "h")
    exchange_out("d", "y", ["TLh%d" % RO, "TLt%d" % RO], T.YP)
    scan(["EYa", "EYb", "ZW", "YSa"], ["YSb"], T.YS[:, NP:V], T.EY[:, NP:V], T.ZW[:, 0:NP], T.YS[:, NP - 1:NP], ALU.add, ALU.add)
    dmas("y", "dys1", ["YSb"], [], [(T.ys[:, NP:V], T.YS[:, NP:V])])
    exchange_in("d", "y", [], T.yp)
    wait("y", list(count.items()))
